import numpy as np, ml_dtypes
CORES = [9,25,41,57]
N = 4
BF = ml_dtypes.bfloat16
def gentries(a):
    return np.ascontiguousarray(a.reshape(8, 16, -1).transpose(0, 2, 1)).reshape(8, -1)
def gtable(e):
    e = np.asarray(e); return np.ascontiguousarray(e.reshape(8, -1, 16).transpose(0, 2, 1)).reshape(128, -1).astype(np.int32)
P, A, M, Q = 65536, 4, 8, 512
S = N * P
def letters(rng, w, n):
    a = np.add.accumulate(w); return np.searchsorted(a[:-1], rng.random(n) * a[-1], side="right")
def places(rng):
    p = rng.integers(0, S + 1, (N, 8, 2, Q)); u = P // 8
    v = rng.integers(0, 8 * N + 1, p.shape) * u + rng.integers(-1, 2, p.shape)
    p = np.sort(np.where(rng.random(p.shape) < 0.25, np.minimum(np.maximum(v, 0), S), p), axis=2)
    k = (8 * np.arange(N)[:, None] + np.arange(8)) * u
    p[:, :, 0, Q - 5] = k; p[:, :, 1, Q - 5] = k + u; p[:, :, :, Q - 4] = S; p[:, :, :, Q - 3] = 0
    p[:, :, 1, Q - 2] = p[:, :, 0, Q - 2]; p[:, :, 0, Q - 1] = 0; p[:, :, 1, Q - 1] = S
    return p
def pack(s, e, p):
    return {"bwt": np.ascontiguousarray(np.asarray(s).reshape(8, N, P).transpose(1, 0, 2)).astype(np.int32), "pats": np.stack([gtable(e[r].reshape(8, M * Q)) for r in range(N)]), "starts": np.stack([gtable(p[r].reshape(8, 2 * Q)) for r in range(N)])}
def bw(t):
    n = len(t); key = np.zeros(n, np.int64); k = 62 // (A - 1).bit_length()
    for i in range(k): key = key * A + np.roll(t, -i)
    while True:
        o = np.argsort(key); ks = key[o]
        v = np.zeros(n, np.int64); v[o[1:]] = np.add.accumulate((ks[1:] != ks[:-1]).astype(np.int64))
        if v.max() == n - 1 or k >= n: break
        key = (v * n + np.roll(v, -k)) * n + np.roll(v, -2 * k); k *= 3
    return t[o - 1]
def setup_inputs(rng):
    s = []; e = rng.integers(0, A, (N, 8, M, Q)); h = Q // 2
    for g in range(8):
        w = np.exp2(rng.integers(0, 4, A)); c = rng.integers(0, A); w[c] += 4 * A
        s.append(np.concatenate([letters(rng, w * np.exp2(rng.integers(0, 3, A)), P) for r in range(N)]))
        e[:, g, :, :h] = np.where(rng.random((N, M, h)) < 0.875, c, e[:, g, :, :h])
    return pack(np.stack(s), e, places(rng))
def setup_inputs_ends(rng):
    i = np.arange(S); s = np.zeros((8, S), np.int64)
    s[0] = i * A // S; s[1] = A - 1 - s[0]; s[2] = i % A; s[3] = rng.integers(0, A - 1, S); s[4] = rng.integers(1, A, S); s[5] = i // P % A
    s[6] = np.where((i % P == 0) | (i % P == P - 1), A - 1, rng.integers(0, A - 1, S)); s[7] = np.where(i == S - 1, A - 1, rng.integers(0, A - 1, S))
    e = rng.integers(0, A, (N, 8, M, Q)); e[..., 0] = 0; e[..., 1] = A - 1; e[..., 2] = 0; e[:, :, 0, 2] = A - 1; e[..., 3] = 0; e[:, :, M - 1, 3] = A - 1
    q = rng.integers(0, N); e[q] = rng.integers(0, A, (8, M, 1)); e[q, 0] = e[q, 0, 0, 0]
    p = places(rng); p[:, :, 0, :4] = 0; p[:, :, 1, :4] = S; p[q, :, 0] = 0; p[q, :, 1] = S
    return pack(s, e, p)
def setup_inputs_one(rng):
    k = (np.arange(8) + rng.integers(0, A)) % A; c = k[None, :, None, None]
    e = np.where(rng.random((N, 8, 1, Q)) < 0.5, c, rng.integers(0, A, (N, 8, M, Q))); e[..., 0] = k[None, :, None]
    return pack(np.repeat(k[:, None], S, axis=1), e, places(rng))
def setup_inputs_text(rng):
    s = []; e = np.zeros((N, 8, M, Q), np.int64); h = Q // 2
    for g in range(8):
        t = np.tile(letters(rng, np.exp2(rng.integers(0, 3, A)), S // 8), 8); t = np.where(rng.random(S) < 0.03125, rng.integers(0, A, S), t); s.append(bw(t))
        e[:, g] = t[(rng.integers(0, S, (N, 1, Q)) + (M - 1 - np.arange(M))[None, :, None]) % S]
    e[..., h:] = np.where(rng.random((N, 8, M, Q - h)) < 0.0625, rng.integers(0, A, (N, 8, M, Q - h)), e[..., h:])
    p = places(rng); p[:, :, 0, :h] = 0; p[:, :, 1, :h] = S
    return pack(np.stack(s), e, p)
def setup_inputs_spread(rng):
    s = np.stack([np.concatenate([letters(rng, np.exp2(-2.0 * rng.permutation(A)), P) for r in range(N)]) for g in range(8)])
    e = np.stack([s[g][rng.integers(0, S, (N, M, Q))] for g in range(8)], axis=1)
    p = places(rng); p[:, :, 1] = np.minimum(p[:, :, 0] + (rng.integers(0, S + 1, (N, 8, Q)) >> rng.integers(0, 20, (N, 8, Q))), S)
    return pack(s, np.where(rng.random((N, 8, 1, Q)) < 0.5, e, rng.integers(0, A, (N, 8, M, Q))), p)
def check_inputs(d):
    bad = [k + " out of range" for k in ("bwt", "pats") if not ((d[k] >= 0) & (d[k] < A)).all()]
    if not ((d["starts"] >= 0) & (d["starts"] <= S)).all(): bad.append("starts out of range")
    p = np.stack([gentries(a) for a in d["starts"]]).reshape(N, 8, 2, Q)
    if (p[:, :, 0] > p[:, :, 1]).any(): bad.append("lo over hi in starts")
    return bad
def reference(bwt, pats, starts):
    s = bwt.transpose(1, 0, 2).reshape(8, S)
    e = np.stack([gentries(pats[r]) for r in range(N)]).reshape(N, 8, M, Q)
    b = np.stack([gentries(starts[r]) for r in range(N)]).reshape(N, 8, 2, Q).astype(np.int64)
    ends = np.zeros((N, 8, 2, Q), np.int64)
    for g in range(8):
        C = np.array([np.count_nonzero(s[g] < c) for c in range(A)]); occ = np.zeros((A, S + 1), np.int64)
        for c in range(A): occ[c, 1:] = np.add.accumulate((s[g] == c).astype(np.int64))
        p = b[:, g]
        for t in range(M):
            c = e[:, g, t][:, None]; p = C[c] + occ[c, p]
        ends[:, g] = p
    return {"y": np.asarray(np.stack([gtable(ends[r].reshape(8, 2 * Q)) for r in range(N)]), np.float32)}

@@ -1,0 +1,398 @@
+import math
+import numpy as np
+from concourse.bass import DstId, RemoteDMATransfer
+from concourse.mybir import AluOpType as A, ActivationFunctionType as F
+
+NR, ST = 4, 8
+KC = 30718 - 2048
+BIG = 12582912.0
+SCRATCH = {
+    "Xb": ("sbuf", [128, 4096], "bfloat16"), "Xe": ("sbuf", [128, 4096], "bfloat16"),
+    "V": ("sbuf", [128, 16392], "int32"), "W": ("sbuf", [128, 4104], "float32"),
+    "wi": ("sbuf", [128, 2048], "int32"),
+    "q0": ("sbuf", [128, 256], "float32"), "q1": ("sbuf", [128, 256], "float32"), "q2": ("sbuf", [128, 256], "float32"),
+    "e0": ("sbuf", [128, 256], "float32"), "e1": ("sbuf", [128, 256], "float32"), "e2": ("sbuf", [128, 256], "float32"),
+    "zz": ("sbuf", [128, 16], "float32"), "kt": ("sbuf", [128, 256], "float16"),
+    "rt": ("sbuf", [128, 16], "float32"), "inc": ("sbuf", [128, 16], "float32"), "exc": ("sbuf", [128, 16], "float32"),
+    "tq": ("sbuf", [128, 8], "float32"),
+    "bs": ("sbuf", [128, 264], "float32"),
+    "dh": ("sbuf", [128, 264], "float16"), "dr": ("sbuf", [128, 264], "float16"), "de": ("sbuf", [128, 264], "float16"),
+    "M1": ("sbuf", [128, 264], "float32"),
+    "M0": ("sbuf", [128, 64], "bfloat16"), "km": ("sbuf", [128, 264], "float32"), "jq": ("sbuf", [128, 264], "int32"),
+    "xi": ("sbuf", [128, 264], "int32"), "xf": ("sbuf", [128, 144], "float32"), "pi": ("sbuf", [128, 1], "int32"),
+    "pk": ("sbuf", [128, 8], "int32"), "pf": ("sbuf", [128, 8], "float32"), "tc": ("sbuf", [128, 40], "float32"),
+    "w4": ("sbuf", [128, 1], "float32"),
+    "E": ("sbuf", [128, 144], "bfloat16"), "ES": ("sbuf", [128, 144], "float16"),
+    "Pm": ("sbuf", [128, 128], "bfloat16"), "Ih": ("sbuf", [128, 128], "float16"), "In": ("sbuf", [128, 128], "float16"),
+    "xg": ("sbuf", [128, 128], "int32"), "BO": ("sbuf", [128, 128], "float32"),
+    "Lt": ("sbuf", [128, 16], "float32"), "m0i": ("sbuf", [128, 128], "int32"), "m0f": ("sbuf", [128, 128], "float32"),
+    "pats_s": ("sbuf", [128, 256], "int32"), "st_s": ("sbuf", [128, 64], "int32"), "cl": ("sbuf", [128, 256], "float32"),
+    "cz": ("sbuf", [128, 32], "int32"), "st4": ("sbuf", [128, 64], "int32"),
+    "psw": ("psum", [128, 512], "float32"), "psh": ("psum", [128, 512], "float32"), "psm": ("psum", [128, 512], "float32"),
+    "psd": ("psum", [128, 512], "float32"), "pa": ("psum", [128, 512], "float32"), "pb": ("psum", [128, 512], "float32"),
+}
+for _k in range(NR):
+    SCRATCH["wl%d" % _k] = ("sbuf", [128, 772], "float16")
+    SCRATCH["to%d" % _k] = ("sbuf", [128, 4], "float32")
+    SCRATCH["vl%d" % _k] = ("sbuf", [128, 512], "uint16")
+for _k in range(6):
+    SCRATCH["dm%d" % _k] = ("sbuf", [128, 128], "float16")
+for _h in range(2):
+    SCRATCH["ps%d" % _h] = ("psum", [128, 512], "float32")
+    SCRATCH["z%d" % _h] = ("sbuf", [128, 32], "int32")
+    SCRATCH["la%d" % _h] = ("sbuf", [128, 32], "int32")
+    SCRATCH["lb%d" % _h] = ("sbuf", [128, 64], "int32")
+    SCRATCH["ua%d" % _h] = ("sbuf", [128, 32], "uint16")
+    SCRATCH["ub%d" % _h] = ("sbuf", [128, 32], "uint16")
+    SCRATCH["um%d" % _h] = ("sbuf", [128, 32], "uint16")
+    SCRATCH["uv%d" % _h] = ("sbuf", [128, 32], "uint16")
+    SCRATCH["r0%d" % _h] = ("sbuf", [128, 512], "bfloat16")
+    SCRATCH["r1%d" % _h] = ("sbuf", [128, 512], "float32")
+    SCRATCH["ya%d" % _h] = ("sbuf", [128, 512], "float16")
+    SCRATCH["yb%d" % _h] = ("sbuf", [128, 512], "float16")
+    SCRATCH["yo%d" % _h] = ("sbuf", [128, 32], "float32")
+SEMAPHORES = ["sv", "sa", "st", "sg", "ls", "gx0", "gx1", "ldp", "yd0", "yd1"] + ["%s%d" % (s, k) for s in "wt" for k in range(NR)] + ["v%d%d" % (k, h) for k in range(NR) for h in range(2)]
+
+
+def rank_program(g, core, T, topo):
+    rank = T.rank_of(core)
+    if rank is None:
+        return
+    peers = [T.cores[(rank + d) % NR] for d in range(1, NR)]
+    S = T.sem
+    cnt, seen = {"sv": 0, "sa": 0, "st": 0, "sg": 0}, {}
+
+    def waits(q, name, deps):
+        for s, n in deps:
+            if seen.get((name, s), 0) < n:
+                q.wait_ge(S[s], n)
+                seen[(name, s)] = n
+
+    def op(q, name, call, args, deps, kw=None):
+        waits(q, name, deps)
+        call(*args, **(kw or {})).then_inc(S[name], 1)
+        cnt[name] += 1
+        return (name, cnt[name])
+
+    vec, act, ten, syn = g.vector, g.scalar, g.tensor, g.sync
+
+    def copy(out, in_, *deps):
+        return op(vec, "sv", vec.tensor_copy, (out, in_), deps)
+
+    def tt(out, a, b, o, *deps):
+        return op(vec, "sv", vec.tensor_tensor, (out, a, b, o), deps)
+
+    def ts(out, a, s1, o1, s2, o2, *deps):
+        if o2 is None:
+            return op(vec, "sv", vec.tensor_scalar, (out, a, s1, None, o1), deps)
+        return op(vec, "sv", vec.tensor_scalar, (out, a, s1, s2, o1, o2), deps)
+
+    def fill(ap, v, *deps):
+        return op(vec, "sv", vec.memset, (ap, v), deps)
+
+    def scan(out, a, b, i, *deps):
+        return op(vec, "sv", vec.tensor_tensor_scan, (out, a, b, i, A.add, A.add), deps)
+
+    def activ(out, in_, f, deps, **kw):
+        return op(act, "sa", act.activation, (out, in_, f), deps, kw)
+
+    def mms(items, deps):
+        waits(ten, "st", deps)
+        for i, (out, l, r, a, b) in enumerate(items):
+            m = ten.matmul(out, l, r, a, b)
+            if i == len(items) - 1:
+                m.then_inc(S.st, 1)
+        cnt["st"] += 1
+        return ("st", cnt["st"])
+
+    def load(h):
+        g.dma_start(T.Xb[64 * h:64 * h + 64, :], T.bwt[:, 32768 * h:32768 * h + 32768]).then_inc(S["gx%d" % h], 16)
+    g.iota(T.pi[:], [[1, 1]], 0, 1).then_inc(S.sg, 1)
+    load(0)
+    g.iota(T.xi[:], [[1, 264]], 0, 0).then_inc(S.sg, 1)
+    load(1)
+    syn.dma_start(T.pats_s[:], T.pats[:]).then_inc(S.ldp, 16)
+    syn.dma_start(T.st_s[:], T.starts[:]).then_inc(S.ldp, 16)
+
+    pk, pf, tc = T.pk, T.pf, T.tc
+
+    def k1(b, i):
+        return b[:, i:i + 1]
+    for i, (sh, mk) in enumerate([(0, 1), (0, 7), (0, 56), (3, 1), (0, 15), (0, 112), (0, 127), (0, 64)]):
+        d = ts(k1(pk, i), T.pi[:], sh, A.logical_shift_right, mk, A.bitwise_and, ("sg", 1))
+    dp = copy(pf[:, 0:8], pk[:, 0:8], d)
+    dw = activ(T.w4[:], k1(pf, 1), F.Exp, [dp], scale=math.log(4.0))
+    dx = copy(T.xf[:], T.xi[:, 0:144], ("sg", 2))
+    ts(k1(tc, 3), k1(pf, 2), 2.0, A.mult, 15.0, A.add, dp)
+    b = ts(k1(tc, 4), k1(pf, 7), 0.125, A.mult, k1(pf, 1), A.add)
+    ts(k1(tc, 5), k1(pf, 5), 15.0, A.add, None, None)
+    b = ts(k1(tc, 6), k1(pf, 2), 2.0, A.mult, k1(tc, 4), A.add, b)
+    dE = ts(T.E[:], T.xf[:], k1(tc, 3), A.is_equal, T.w4[:], A.mult, b, dx, dw)
+    dP = ts(T.Pm[:], T.xf[:, 0:128], k1(tc, 6), A.is_equal, None, None, b)
+    mine = T["wl%d" % rank]
+
+    def constants_0():
+        fill(T.zz[:], 0.0)
+        fill(T.V[:, 16384:16392], 9)
+        fill(T.W[:, 4096:4104], -2048.0)
+        fill(T.e0[:], -BIG)
+        fill(T["to%d" % rank][:, 3:4], 0.0)
+        ts(mine[:, 0:772:257], T.xi[:, 0:4], 0.0, A.mult, -2048.0, A.add)
+
+    def constants_1():
+        a = ts(T.xg[:], T.xi[:, 0:128], 112, A.bitwise_and, None, None)
+        c = ts(T.m0i[:, 0:64], T.xi[:, 0:64], 2, A.logical_shift_right, None, None)
+        d = ts(T.m0i[:, 64:128], T.xi[:, 0:64], 3, A.bitwise_and, None, None)
+        ts(T.Ih[:], T.xf[:, 0:128], k1(pf, 6), A.is_equal, None, None)
+        ts(T.BO[:], T.xg[:], k1(pf, 5), A.is_equal, 1.0 / 2048, A.mult, a)
+        c = ts(T.m0f[:, 0:64], T.m0i[:, 0:64], k1(pf, 4), A.is_gt, None, None, c)
+        d = ts(T.m0f[:, 64:128], T.m0i[:, 64:128], 1.0, A.add, None, None, d)
+        ts(T.In[:], T.xf[:, 0:128], k1(pf, 6), A.is_equal, -1.0, A.mult)
+        a = tt(T.m0f[:, 0:64], T.m0f[:, 0:64], T.m0f[:, 64:128], A.mult, d)
+        ts(T.kt[:], T.xi[:, 0:256], 16.0, A.mult, -8192.0, A.add)
+        ts(T.M0[:], T.m0f[:, 0:64], -1.0, A.add, None, None, a)
+        ts(T.ES[:], T.xf[:], k1(tc, 5), A.is_equal, 4.0, A.mult)
+        ts(T.Lt[:], T.xf[:, 0:16], k1(pf, 4), A.is_gt, None, None)
+
+    def constants_2():
+        a = ts(T.jq[:], T.xi[:], 15, A.bitwise_and, None, None)
+        ts(k1(tc, 8), k1(pf, 3), -448.0, A.mult, 448.0, A.add)
+        for i, v in enumerate([9, 8]):
+            ts(k1(tc, 10 + i), k1(pf, 4), float(v), A.is_equal, 256.0, A.mult)
+        for i, v in enumerate([11, 10, 13, 12]):
+            a = ts(k1(tc, 12 + i), k1(pf, 4), float(v), A.is_equal, None, None)
+        b = tt(k1(tc, 18), k1(tc, 8), k1(pf, 0), A.mult, a)
+        ts(T.km[:], T.jq[:], k1(pf, 4), A.is_equal, -6144.0, A.mult)
+        b = tt(k1(tc, 19), k1(tc, 8), k1(tc, 18), A.subtract, b)
+        c = ts(tc[:, 22:24], tc[:, 12:14], -2048.0, A.mult, 2048.0, A.add)
+        b = tt(tc[:, 20:22], tc[:, 18:20], tc[:, 10:12], A.add, b)
+        d = ts(tc[:, 24:26], tc[:, 14:16], 2046.0, A.mult, None, None)
+        e = tt(tc[:, 26:28], tc[:, 12:14], tc[:, 14:16], A.subtract)
+        ts(tc[:, 28:30], tc[:, 14:16], 2048.0, A.mult, None, None)
+        f = ts(tc[:, 30:32], tc[:, 20:22], -1025.0, A.mult, None, None, b)
+        d = tt(tc[:, 22:24], tc[:, 22:24], tc[:, 24:26], A.add, c, d)
+        for i, col in enumerate([20, 26, 28]):
+            for par in range(2):
+                b = ts(T["dm%d" % (2 * i + par)][:], T.xf[:, 0:128], k1(pf, 6), A.is_equal, k1(tc, col + par), A.mult, f)
+        d = tt(tc[:, 32:34], tc[:, 22:24], tc[:, 30:32], A.add, d, f)
+        for par in range(2):
+            end = 257 if par == 0 else 256
+            ts(T.km[:, par:end:2], T.km[:, par:end:2], k1(tc, 32 + par), A.add, None, None, d)
+
+    def constants_3():
+        waits(vec, "sv", [("ldp", 32)])
+        ts(T.st4[:], T.st_s[:], 4.0, A.mult, None, None)
+        d = ts(T.cz[:], T.pats_s[:, 0:32], 1048577.0, A.mult, None, None)
+        for h in range(2):
+            ts(T["uv%d" % h][:], T.st_s[:, 32 * h:32 * h + 32], 1.0 / 16, A.mult, -15.0 / 32, A.add)
+        ts(T.cl[:], T.pats_s[:], 1048577.0, A.mult, -4.0 * KC, A.add)
+        return d
+
+    def rows(h, *deps):
+        return ts(T["um%d" % h][:], T["z%d" % h][:], 2.0 ** -14, A.mult, 2.0 ** -15 - 0.5, A.add, *deps)
+
+    def parts(h):
+        ts(T["lb%d" % h][:, 0:32], T["z%d" % h][:], 6, A.logical_shift_right, 255, A.bitwise_and)
+        return ts(T["lb%d" % h][:, 32:64], T["z%d" % h][:], 10, A.logical_shift_right, 0x1F00, A.bitwise_and)
+
+    def list_w(h, b):
+        return tt(T["ub%d" % h][:], T["lb%d" % h][:, 0:32], T["lb%d" % h][:, 32:64], A.add, b)
+
+    def list_q(h):
+        return ts(T["la%d" % h][:], T["z%d" % h][:], 63, A.bitwise_and, None, None)
+
+    def list0(h, l):
+        return activ(T["ua%d" % h][:], T["la%d" % h][:], F.Copy, [l])
+
+    def mask0(h, u):
+        return activ(T["r0%d" % h][:], T.M0[:].indirect(T["ua%d" % h][:]), F.Copy, [u])
+
+    def mask1(h, m, *deps):
+        return activ(T["r1%d" % h][:], T.M1[:, 0:257].indirect(T["um%d" % h][:]), F.Copy, [m] + list(deps))
+
+    constants_1()
+    dK = constants_3()
+    ld = [("gx0", 16), ("gx1", 16)]
+
+    def pack(h, bank):
+        sl = slice(64 * h, 64 * h + 64)
+        return mms([(T[bank][:, 0:256], T.E[sl, 15 - q:143 - q], T.Xb[sl, q:4096:16], q == 0, q == 15) for q in range(16)], [dE, ld[h]])
+
+    pkd = [pack(0, "psw")]
+    for j in range(4):
+        sl = slice(1024 * j, 1024 * (j + 1))
+        e = activ(T.Xe[:, sl], T.Xb[:, sl], F.Exp, ld, scale=-math.log(64.0))
+        hd = mms([(T.psh[:, 64 * j:64 * j + 64], T.Pm[:], T.Xe[:, 1024 * j + q:1024 * (j + 1):16], q == 0, q == 15) for q in range(16)], [dP, e])
+    pkd.append(pack(1, "pa"))
+    dq = []
+    for c in range(3):
+        dq.append(activ(T["q%d" % c][:], T.psh[:, 0:256], F.Copy, [hd], scale=64.0 ** c, bias=BIG))
+        if c < 2:
+            activ(T["e%d" % (c + 1)][:], T["q%d" % c][:], F.Copy, [dq[c]], scale=-64.0, bias=63 * BIG)
+
+    ne = len(topo.engines(core, peers[0]))
+
+    def send(ap, sem, deps):
+        waits(g, "gq", deps)
+        ids = [DstId(rid=topo.addr(p)[0], pnc=topo.addr(p)[1]) for p in peers]
+        g.remote_dma_fused([RemoteDMATransfer(dst_ids=ids, dma_engine_mask=topo.mask(core, peers[0]), remote_sem=S[sem], srcs=[ap], dsts=[ap for _ in peers])], local_sem=S.ls)
+
+    def words(b, r, h):
+        return T[b][:, 256 * h:256 * h + 256] if b != "wi" else T.wi[:, 512 * r + 256 * h:512 * r + 256 * h + 256]
+
+    def letter(r, h, k):
+        o = 4096 * r + 2048 * h + 256 * k
+        return T.V[:, o:o + 256]
+
+    def unpack(r, h, k, dep):
+        ts(letter(r, h, k), words("wi", r, h), 2 * k, A.logical_shift_right, 3, A.bitwise_and, dep)
+
+    def top(r, h, *deps):
+        return activ(letter(r, h, 7), words("vl%d" % r, r, h), F.Copy, deps, scale=2.0 ** -14, bias=2.0 ** -15 - 0.5)
+
+    def count(r, c):
+        return T["wl%d" % r][:, 257 * c:257 * c + 256]
+
+    def left(r, bank, deps):
+        return mms([(T[bank][:, 0:256], T.Ih[:], T.kt[:], True, False)] + [(T[bank][:, 0:256], T.In[:], count(r, c), False, c == 2) for c in range(3)], deps)
+
+    def store(r, bank, m, *deps):
+        for c in range(4):
+            e = activ(T.W[:, 1024 * c + 256 * r:1024 * c + 256 * r + 256], count(r, c) if c < 3 else T[bank][:, 0:256], F.Copy, deps if c < 3 else [m])
+        return e
+
+    zr = [tt(T["z%d" % h][:], T.st4[:, 32 * h:32 * h + 32], T.cz[:], A.add, dK) for h in range(2)]
+    um = [rows(h, zr[h]) for h in range(2)]
+    pb = [parts(h) for h in range(2)]
+    la = [list_q(h) for h in range(2)]
+    lb = [list_w(h, pb[h]) for h in range(2)]
+    constants_0()
+    constants_2()
+
+    own, cw = [], []
+
+    def letters(h, bank, n):
+        vl = words("vl%d" % rank, rank, h)
+        cw.append(copy(vl, T[bank][:, 0:256], pkd[h]))
+        send(vl, "v%d%d" % (rank, h), [cw[h]])
+        own.append(copy(words("wi", rank, h), T[bank][:, 0:256]))
+        for k in range(n):
+            unpack(rank, h, k, own[h])
+
+    order = [(rank + NR - k) % NR for k in range(1, NR)]
+    jobs = [(r, h, k) for h in range(2) for r in order for k in range(7)]
+    at = {}
+
+    def work(n):
+        for r, h, k in jobs[:n]:
+            unpack(r, h, k, at[r, h])
+        del jobs[:n]
+
+    def landed(r, h):
+        at[r, h] = activ(words("wi", r, h), words("vl%d" % r, r, h), F.Copy, [("v%d%d" % (r, h), ne)])
+
+    letters(0, "psw", 8)
+    for c in range(3):
+        s = scan(mine[:, 257 * c + 1:257 * c + 257], T["q%d" % c][:], T["e%d" % c][:], -2048.0, dq[c])
+    to = ts(T["to%d" % rank][:, 0:3], mine[:, 256:771:257], 2048.0, A.add, None, None, s)
+    send(T["to%d" % rank][:], "t%d" % rank, [to])
+    u = [list0(h, la[h]) for h in range(2)]
+    mk = [[mask0(h, u[h]), None] for h in range(2)]
+    landed(order[0], 0)
+    letters(1, "pa", 7)
+    send(mine[:], "w%d" % rank, [s])
+
+    landed(order[1], 0)
+    landed(order[2], 0)
+    top(rank, 1, cw[1])
+    m0 = left(rank, "psw", [s, own[0]])
+    store(rank, "psw", m0, s)
+    for r in order:
+        top(r, 0, at[r, 0])
+
+    work(6)
+    copy(T.rt[:, rank:12:4], T["to%d" % rank][:, 0:3], to)
+    for r in order:
+        a = copy(T.rt[:, r:12:4], T["to%d" % r][:, 0:3], ("t%d" % r, ne))
+    work(1)
+    a = tt(T.tq[:, 0:4], T.rt[:, 0:4], T.rt[:, 4:8], A.add, a)
+    work(1)
+    a = tt(T.tq[:, 4:8], T.tq[:, 0:4], T.rt[:, 8:12], A.add, a)
+    work(1)
+    a = ts(T.rt[:, 12:16], T.tq[:, 4:8], -1.0, A.mult, 4096.0, A.add, a)
+    work(1)
+    a = scan(T.inc[:], T.rt[:], T.zz[:], 131200.0, a)
+    work(1)
+    b = copy(T.bs[:, 256:257], T.inc[:, 15:16], a)
+    a = tt(T.exc[:], T.inc[:], T.rt[:], A.subtract, a)
+    for k in range(16):
+        ba = activ(T.bs[:, 16 * k:16 * k + 16], T.Lt[:], F.Identity, [a], bias=k1(T.exc, k), scale=k1(T.rt, k))
+    m = mms([(T.psm[:, 0:257], T.BO[:], T.bs[:, 0:257], True, True)], [b, ba])
+    landed(order[0], 1)
+    n = 257
+    a = activ(T.dh[:, 0:n], T.psm[:, 0:n], F.Copy, [m], scale=1.0, bias=2.0 ** -12 - 0.5)
+    work(12)
+    a = tt(T.dr[:, 0:n], T.psm[:, 0:n], T.dh[:, 0:n], A.subtract, a)
+    landed(order[1], 1)
+    a = activ(T.de[:, 0:n], T.dr[:, 0:n], F.Copy, [a], scale=2048.0, bias=2047.75)
+    for par in range(2):
+        m = mms([(T.psd[:, par:par + 129] if par == 0 else T.psm[:, 0:128], T["dm%d" % (2 * i + par)][:], T[buf][:, par:257:2], i == 0, i == 2) for i, buf in enumerate(("dh", "de", "dr"))], [a])
+    work(4)
+    for par in range(2):
+        n, end = 129 - par, 257 if par == 0 else 256
+        dM = tt(T.M1[:, par:end:2], (T.psd if par == 0 else T.psm)[:, 0:n], T.km[:, par:end:2], A.add, m)
+    landed(order[2], 1)
+    banks = ("psh", "pa", "pb")
+    lf = [left(r, b, [("w%d" % r, ne), own[1], dq[2]]) for r, b in zip(order, banks)]
+    for i, r in enumerate(order):
+        dT = top(r, 1, at[r, 1])
+        if i == 2:
+            mk[0][1] = mask1(0, um[0], dM)
+        dW = store(r, banks[i], lf[i], ("w%d" % r, ne))
+    mk[1][1] = mask1(1, um[1], dM)
+    work(len(jobs))
+    dV = ("sv", cnt["sv"])
+
+    res, du = [None, None], [dT, dT]
+
+    def sums(h, y, first, deps):
+        items = [(T["ps%d" % h][:, 0:32], T.ES[:, 15 - q:143 - q], T[y][:, q::16], first and q == 0, (not first) and q == 15) for q in range(16)]
+        return mms(items, deps)
+
+    def y1(h, first):
+        e = tt(T["ya%d" % h][:], T.V[:].indirect(T["uv%d" % h][:]), T["r0%d" % h][:], A.is_equal, du[h], mk[h][0], dV)
+        return sums(h, "ya%d" % h, first, [e])
+
+    def y2(h, first):
+        e = tt(T["yb%d" % h][:], T.W[:, 0:4097].indirect(T["ub%d" % h][:]), T["r1%d" % h][:], A.max, lb[h], mk[h][1], dW)
+        return sums(h, "yb%d" % h, first, [e, du[h]])
+
+    def head(h, t):
+        z = tt(T["z%d" % h][:], T["ps%d" % h][:, 0:32], T.cl[:, 32 * t:32 * t + 32], A.add, res[h])
+        mk[h][1] = mask1(h, rows(h, z))
+        u = list0(h, list_q(h))
+        du[h] = activ(T["uv%d" % h][:], T["ps%d" % h][:, 0:32], F.Copy, [res[h]], scale=1.0 / 64, bias=-KC / 16.0 - 15.0 / 32)
+        mk[h][0] = mask0(h, u)
+
+    def tail(h):
+        lb[h] = list_w(h, parts(h))
+
+    y1(0, True)
+    res[0] = y2(0, False)
+    y2(1, True)
+    for t in range(1, ST):
+        head(0, t)
+        res[1] = y1(1, False)
+        tail(0)
+        y2(0, True)
+        head(1, t)
+        res[0] = y1(0, False)
+        tail(1)
+        y2(1, True)
+    res[1] = y1(1, False)
+    for h in range(2):
+        e = ts(T["yo%d" % h][:], T["ps%d" % h][:, 0:32], 0.25, A.mult, -float(KC), A.add, res[h])
+        waits(syn, "sy", [e])
+        syn.dma_start(T.y[:, 32 * h:32 * h + 32], T["yo%d" % h][:]).then_inc(S["yd%d" % h], 16)
+    waits(syn, "sy", [("yd0", 16), ("yd1", 16)])
+    g.wait_ge(S.ls, 4 * ne)

@@ -1,32 +1,32 @@
 import math
 import numpy as np
 from concourse.bass import DstId, RemoteDMATransfer
-from concourse.mybir import AluOpType as A, ActivationFunctionType as F
+from concourse.mybir import AluOpType as A, ActivationFunctionType as F, AxisListType as AX
 
 NR, ST = 4, 8
 KC = 30718 - 2048
 BIG = 12582912.0
 SCRATCH = {
     "Xb": ("sbuf", [128, 4096], "bfloat16"), "Xe": ("sbuf", [128, 4096], "bfloat16"),
-    "V": ("sbuf", [128, 16392], "int32"), "W": ("sbuf", [128, 4104], "float32"),
-    "wi": ("sbuf", [128, 2048], "int32"),
+    "V": ("sbuf", [128, 16392], "int32"), "W": ("sbuf", [128, 13312], "int32"), "cw": ("sbuf", [128, 256], "int32"),
     "q0": ("sbuf", [128, 256], "float32"), "q1": ("sbuf", [128, 256], "float32"), "q2": ("sbuf", [128, 256], "float32"),
     "e0": ("sbuf", [128, 256], "float32"), "e1": ("sbuf", [128, 256], "float32"), "e2": ("sbuf", [128, 256], "float32"),
     "zz": ("sbuf", [128, 16], "float32"), "kt": ("sbuf", [128, 256], "float16"),
     "rt": ("sbuf", [128, 16], "float32"), "inc": ("sbuf", [128, 16], "float32"), "exc": ("sbuf", [128, 16], "float32"),
-    "tq": ("sbuf", [128, 8], "float32"),
+    "adj": ("sbuf", [128, 4], "float32"),
     "bs": ("sbuf", [128, 264], "float32"),
     "dh": ("sbuf", [128, 264], "float16"), "dr": ("sbuf", [128, 264], "float16"), "de": ("sbuf", [128, 264], "float16"),
     "M1": ("sbuf", [128, 264], "float32"),
     "M0": ("sbuf", [128, 64], "bfloat16"), "km": ("sbuf", [128, 264], "float32"), "jq": ("sbuf", [128, 264], "int32"),
-    "xi": ("sbuf", [128, 264], "int32"), "xf": ("sbuf", [128, 144], "float32"), "pi": ("sbuf", [128, 1], "int32"),
+    "xi": ("sbuf", [128, 264], "int32"), "xf": ("sbuf", [128, 264], "float32"), "pi": ("sbuf", [128, 1], "int32"),
     "pk": ("sbuf", [128, 8], "int32"), "pf": ("sbuf", [128, 8], "float32"), "tc": ("sbuf", [128, 40], "float32"),
     "w4": ("sbuf", [128, 1], "float32"),
     "E": ("sbuf", [128, 144], "bfloat16"), "ES": ("sbuf", [128, 144], "float16"),
     "Pm": ("sbuf", [128, 128], "bfloat16"), "Ih": ("sbuf", [128, 128], "float16"), "In": ("sbuf", [128, 128], "float16"),
     "xg": ("sbuf", [128, 128], "int32"), "BO": ("sbuf", [128, 128], "float32"),
     "Lt": ("sbuf", [128, 16], "float32"), "m0i": ("sbuf", [128, 128], "int32"), "m0f": ("sbuf", [128, 128], "float32"),
-    "pats_s": ("sbuf", [128, 256], "int32"), "st_s": ("sbuf", [128, 64], "int32"), "cl": ("sbuf", [128, 256], "float32"),
+    "pats_s": ("sbuf", [128, 256], "int32"), "st_s": ("sbuf", [128, 64], "int32"), "cm": ("sbuf", [128, 256], "float32"),
+    "cq": ("sbuf", [128, 256], "float16"),
     "cz": ("sbuf", [128, 32], "int32"), "st4": ("sbuf", [128, 64], "int32"),
     "psw": ("psum", [128, 512], "float32"), "psh": ("psum", [128, 512], "float32"), "psm": ("psum", [128, 512], "float32"),
     "psd": ("psum", [128, 512], "float32"), "pa": ("psum", [128, 512], "float32"), "pb": ("psum", [128, 512], "float32"),
@@ -34,14 +34,13 @@ SCRATCH = {
 for _k in range(NR):
     SCRATCH["wl%d" % _k] = ("sbuf", [128, 772], "float16")
     SCRATCH["to%d" % _k] = ("sbuf", [128, 4], "float32")
-    SCRATCH["vl%d" % _k] = ("sbuf", [128, 512], "uint16")
 for _k in range(6):
     SCRATCH["dm%d" % _k] = ("sbuf", [128, 128], "float16")
 for _h in range(2):
     SCRATCH["ps%d" % _h] = ("psum", [128, 512], "float32")
     SCRATCH["z%d" % _h] = ("sbuf", [128, 32], "int32")
     SCRATCH["la%d" % _h] = ("sbuf", [128, 32], "int32")
-    SCRATCH["lb%d" % _h] = ("sbuf", [128, 64], "int32")
+    SCRATCH["lb%d" % _h] = ("sbuf", [128, 32], "int32")
     SCRATCH["ua%d" % _h] = ("sbuf", [128, 32], "uint16")
     SCRATCH["ub%d" % _h] = ("sbuf", [128, 32], "uint16")
     SCRATCH["um%d" % _h] = ("sbuf", [128, 32], "uint16")
@@ -52,12 +51,47 @@ for _h in range(2):
     SCRATCH["yb%d" % _h] = ("sbuf", [128, 512], "float16")
     SCRATCH["yo%d" % _h] = ("sbuf", [128, 32], "float32")
 SEMAPHORES = ["sv", "sa", "st", "sg", "ls", "gx0", "gx1", "ldp", "yd0", "yd1"] + ["%s%d" % (s, k) for s in "wt" for k in range(NR)] + ["v%d%d" % (k, h) for k in range(NR) for h in range(2)]
+SEMAPHORES += ["hin0", "hin1"] + ["x%d" % k for k in range(NR)]
+CUT = 514
+
+
+def helper_of(core, T, topo):
+    return [c for c in topo.cores_of(core) if topo.die(c) != topo.die(core) and T.rank_of(c) is None][0]
+
+
+def write(g, T, topo, cores, mask, ap, sem):
+    ids = [DstId(rid=topo.addr(p)[0], pnc=topo.addr(p)[1]) for p in cores]
+    g.remote_dma_fused([RemoteDMATransfer(dst_ids=ids, dma_engine_mask=mask, remote_sem=T.sem[sem], srcs=[ap], dsts=[ap for _ in cores])], local_sem=T.sem.ls)
+    return bin(mask).count("1")
+
+
+def words(T, r, h):
+    return T.W[:, 1024 + 512 * r + 256 * h:1280 + 512 * r + 256 * h]
+
+
+def handed(T, rank):
+    return [(words(T, rank, 1), "v%d1" % rank), (T["wl%d" % rank][:, CUT:772], "x%d" % rank)]
+
+
+def inner_mask(core, helper, peer, topo):
+    return topo.mask(core, helper) & ~topo.mask(core, peer)
+
+
+def hand_on(g, core, T, topo):
+    for rank, owner in enumerate(T.cores):
+        if helper_of(owner, T, topo) == core:
+            peers = [T.cores[(rank + d) % NR] for d in range(1, NR)]
+            n = 0
+            for i, (ap, sem) in enumerate(handed(T, rank)):
+                g.wait_ge(T.sem["hin%d" % i], bin(inner_mask(owner, core, peers[0], topo)).count("1"))
+                n += write(g, T, topo, peers, topo.mask(core, peers[0]), ap, sem)
+            g.wait_ge(T.sem.ls, n)
 
 
 def rank_program(g, core, T, topo):
     rank = T.rank_of(core)
     if rank is None:
-        return
+        return hand_on(g, core, T, topo)
     peers = [T.cores[(rank + d) % NR] for d in range(1, NR)]
     S = T.sem
     cnt, seen = {"sv": 0, "sa": 0, "st": 0, "sg": 0}, {}
@@ -96,6 +130,9 @@ def rank_program(g, core, T, topo):
     def activ(out, in_, f, deps, **kw):
         return op(act, "sa", act.activation, (out, in_, f), deps, kw)
 
+    def affine(out, in_, scale, bias, *deps):
+        return activ(out, in_, F.Copy, deps, scale=scale, bias=bias)
+
     def mms(items, deps):
         waits(ten, "st", deps)
         for i, (out, l, r, a, b) in enumerate(items):
@@ -105,150 +142,165 @@ def rank_program(g, core, T, topo):
         cnt["st"] += 1
         return ("st", cnt["st"])
 
-    def load(h):
+    op(g, "sg", g.iota, (T.pi[:], [[1, 1]], 0, 1), [])
+    for h in range(2):
         g.dma_start(T.Xb[64 * h:64 * h + 64, :], T.bwt[:, 32768 * h:32768 * h + 32768]).then_inc(S["gx%d" % h], 16)
-    g.iota(T.pi[:], [[1, 1]], 0, 1).then_inc(S.sg, 1)
-    load(0)
-    g.iota(T.xi[:], [[1, 264]], 0, 0).then_inc(S.sg, 1)
-    load(1)
+
+    def blank(a, b):
+        return op(g, "sg", g.iota, (T.W[:, a:b], [[0, b - a]], 0, 0), [])
+
+    blank(3072, 4096)
+    blank(5120, 5632)
     syn.dma_start(T.pats_s[:], T.pats[:]).then_inc(S.ldp, 16)
     syn.dma_start(T.st_s[:], T.starts[:]).then_inc(S.ldp, 16)
 
     pk, pf, tc = T.pk, T.pf, T.tc
+    mine = T["wl%d" % rank]
 
     def k1(b, i):
         return b[:, i:i + 1]
+
+    a = fill(T.km[:], 0.5)
     for i, (sh, mk) in enumerate([(0, 1), (0, 7), (0, 56), (3, 1), (0, 15), (0, 112), (0, 127), (0, 64)]):
         d = ts(k1(pk, i), T.pi[:], sh, A.logical_shift_right, mk, A.bitwise_and, ("sg", 1))
+    dx = scan(T.xf[:], T.km[:], T.km[:], -1.0, a)
     dp = copy(pf[:, 0:8], pk[:, 0:8], d)
     dw = activ(T.w4[:], k1(pf, 1), F.Exp, [dp], scale=math.log(4.0))
-    dx = copy(T.xf[:], T.xi[:, 0:144], ("sg", 2))
+    di = copy(T.xi[:], T.xf[:], dx)
     ts(k1(tc, 3), k1(pf, 2), 2.0, A.mult, 15.0, A.add, dp)
     b = ts(k1(tc, 4), k1(pf, 7), 0.125, A.mult, k1(pf, 1), A.add)
     ts(k1(tc, 5), k1(pf, 5), 15.0, A.add, None, None)
+    dI = ts(T.Ih[:], T.xf[:, 0:128], k1(pf, 6), A.is_equal, None, None)
     b = ts(k1(tc, 6), k1(pf, 2), 2.0, A.mult, k1(tc, 4), A.add, b)
-    dE = ts(T.E[:], T.xf[:], k1(tc, 3), A.is_equal, T.w4[:], A.mult, b, dx, dw)
+    a = ts(T.xg[:], T.xi[:, 0:128], 112, A.bitwise_and, None, None, di)
+    c = ts(T.m0i[:, 0:64], T.xi[:, 0:64], 2, A.logical_shift_right, None, None)
+    d = ts(T.m0i[:, 64:128], T.xi[:, 0:64], 3, A.bitwise_and, None, None)
     dP = ts(T.Pm[:], T.xf[:, 0:128], k1(tc, 6), A.is_equal, None, None, b)
-    mine = T["wl%d" % rank]
+    ts(T.BO[:], T.xg[:], k1(pf, 5), A.is_equal, 1.0 / 2048, A.mult, a)
+    c = ts(T.m0f[:, 0:64], T.m0i[:, 0:64], k1(pf, 4), A.is_gt, None, None, d)
+    d = ts(T.m0f[:, 64:128], T.m0i[:, 64:128], 1.0, A.add, None, None)
+    ts(T.ES[:], T.xf[:, 0:144], k1(tc, 5), A.is_equal, 2.0 ** -12, A.mult)
+    a = tt(T.m0f[:, 0:64], T.m0f[:, 0:64], T.m0f[:, 64:128], A.mult, d)
+    ts(T.Lt[:], T.xf[:, 0:16], k1(pf, 4), A.is_gt, None, None)
+    ts(T.jq[:], T.xi[:], 15, A.bitwise_and, None, None)
+    d0 = ts(T.M0[:], T.m0f[:, 0:64], -1.0, A.add, None, None, a)
+    dE = ts(T.E[:], T.xf[:, 0:144], k1(tc, 3), A.is_equal, T.w4[:], A.mult, dw)
 
-    def constants_0():
-        fill(T.zz[:], 0.0)
-        fill(T.V[:, 16384:16392], 9)
-        fill(T.W[:, 4096:4104], -2048.0)
-        fill(T.e0[:], -BIG)
-        fill(T["to%d" % rank][:, 3:4], 0.0)
-        ts(mine[:, 0:772:257], T.xi[:, 0:4], 0.0, A.mult, -2048.0, A.add)
+    affine(T.st4[:], T.st_s[:], 4.0, 0.0, ("ldp", 32))
+    dK = affine(T.cz[:], T.pats_s[:, 0:32], 1048577.0, 0.0)
+    for h in range(2):
+        affine(T["uv%d" % h][:], T.st_s[:, 32 * h:32 * h + 32], 1.0 / 16, -15.0 / 32)
+    affine(T.cm[:], T.pats_s[:], 64.0, 2.0 ** -15 - 0.5 - KC / 4096.0)
+    affine(T.cq[:], T.pats_s[:], 2.0 ** -14, 0.0)
+    dC = affine(T.cw[:], T.pats_s[:], 256.0, 0.0)
+    affine(T.e0[:], T.xf[:, 0:256], 0.0, -BIG, dx)
+    affine(T.In[:], T.Ih[:], -1.0, 0.0, dI)
 
-    def constants_1():
-        a = ts(T.xg[:], T.xi[:, 0:128], 112, A.bitwise_and, None, None)
-        c = ts(T.m0i[:, 0:64], T.xi[:, 0:64], 2, A.logical_shift_right, None, None)
-        d = ts(T.m0i[:, 64:128], T.xi[:, 0:64], 3, A.bitwise_and, None, None)
-        ts(T.Ih[:], T.xf[:, 0:128], k1(pf, 6), A.is_equal, None, None)
-        ts(T.BO[:], T.xg[:], k1(pf, 5), A.is_equal, 1.0 / 2048, A.mult, a)
-        c = ts(T.m0f[:, 0:64], T.m0i[:, 0:64], k1(pf, 4), A.is_gt, None, None, c)
-        d = ts(T.m0f[:, 64:128], T.m0i[:, 64:128], 1.0, A.add, None, None, d)
-        ts(T.In[:], T.xf[:, 0:128], k1(pf, 6), A.is_equal, -1.0, A.mult)
-        a = tt(T.m0f[:, 0:64], T.m0f[:, 0:64], T.m0f[:, 64:128], A.mult, d)
-        ts(T.kt[:], T.xi[:, 0:256], 16.0, A.mult, -8192.0, A.add)
-        ts(T.M0[:], T.m0f[:, 0:64], -1.0, A.add, None, None, a)
-        ts(T.ES[:], T.xf[:], k1(tc, 5), A.is_equal, 4.0, A.mult)
-        ts(T.Lt[:], T.xf[:, 0:16], k1(pf, 4), A.is_gt, None, None)
-
-    def constants_2():
-        a = ts(T.jq[:], T.xi[:], 15, A.bitwise_and, None, None)
-        ts(k1(tc, 8), k1(pf, 3), -448.0, A.mult, 448.0, A.add)
-        for i, v in enumerate([9, 8]):
-            ts(k1(tc, 10 + i), k1(pf, 4), float(v), A.is_equal, 256.0, A.mult)
-        for i, v in enumerate([11, 10, 13, 12]):
-            a = ts(k1(tc, 12 + i), k1(pf, 4), float(v), A.is_equal, None, None)
-        b = tt(k1(tc, 18), k1(tc, 8), k1(pf, 0), A.mult, a)
-        ts(T.km[:], T.jq[:], k1(pf, 4), A.is_equal, -6144.0, A.mult)
-        b = tt(k1(tc, 19), k1(tc, 8), k1(tc, 18), A.subtract, b)
-        c = ts(tc[:, 22:24], tc[:, 12:14], -2048.0, A.mult, 2048.0, A.add)
-        b = tt(tc[:, 20:22], tc[:, 18:20], tc[:, 10:12], A.add, b)
-        d = ts(tc[:, 24:26], tc[:, 14:16], 2046.0, A.mult, None, None)
-        e = tt(tc[:, 26:28], tc[:, 12:14], tc[:, 14:16], A.subtract)
-        ts(tc[:, 28:30], tc[:, 14:16], 2048.0, A.mult, None, None)
-        f = ts(tc[:, 30:32], tc[:, 20:22], -1025.0, A.mult, None, None, b)
-        d = tt(tc[:, 22:24], tc[:, 22:24], tc[:, 24:26], A.add, c, d)
-        for i, col in enumerate([20, 26, 28]):
-            for par in range(2):
-                b = ts(T["dm%d" % (2 * i + par)][:], T.xf[:, 0:128], k1(pf, 6), A.is_equal, k1(tc, col + par), A.mult, f)
-        d = tt(tc[:, 32:34], tc[:, 22:24], tc[:, 30:32], A.add, d, f)
-        for par in range(2):
-            end = 257 if par == 0 else 256
-            ts(T.km[:, par:end:2], T.km[:, par:end:2], k1(tc, 32 + par), A.add, None, None, d)
-
-    def constants_3():
-        waits(vec, "sv", [("ldp", 32)])
-        ts(T.st4[:], T.st_s[:], 4.0, A.mult, None, None)
-        d = ts(T.cz[:], T.pats_s[:, 0:32], 1048577.0, A.mult, None, None)
-        for h in range(2):
-            ts(T["uv%d" % h][:], T.st_s[:, 32 * h:32 * h + 32], 1.0 / 16, A.mult, -15.0 / 32, A.add)
-        ts(T.cl[:], T.pats_s[:], 1048577.0, A.mult, -4.0 * KC, A.add)
-        return d
+    ts(k1(tc, 8), k1(pf, 3), -448.0, A.mult, 448.0, A.add)
+    for i, v in enumerate([9, 8]):
+        ts(k1(tc, 10 + i), k1(pf, 4), float(v), A.is_equal, 256.0, A.mult)
+    for i, v in enumerate([11, 10, 13, 12]):
+        a = ts(k1(tc, 12 + i), k1(pf, 4), float(v), A.is_equal, None, None)
+    ts(T.km[:], T.jq[:], k1(pf, 4), A.is_equal, -6144.0, A.mult, d0)
+    b = tt(k1(tc, 18), k1(tc, 8), k1(pf, 0), A.mult, a)
+    c = ts(tc[:, 22:24], tc[:, 12:14], -2048.0, A.mult, 2048.0, A.add)
+    d = ts(tc[:, 24:26], tc[:, 14:16], 2046.0, A.mult, None, None)
+    b = tt(k1(tc, 19), k1(tc, 8), k1(tc, 18), A.subtract, b)
+    tt(tc[:, 26:28], tc[:, 12:14], tc[:, 14:16], A.subtract)
+    ts(tc[:, 28:30], tc[:, 14:16], 2048.0, A.mult, None, None)
+    b = tt(tc[:, 20:22], tc[:, 18:20], tc[:, 10:12], A.add, b)
+    d = tt(tc[:, 22:24], tc[:, 22:24], tc[:, 24:26], A.add, d)
+    fill(T.zz[:], 0.0)
+    f = ts(tc[:, 30:32], tc[:, 20:22], -1025.0, A.mult, None, None, b)
 
     def rows(h, *deps):
         return ts(T["um%d" % h][:], T["z%d" % h][:], 2.0 ** -14, A.mult, 2.0 ** -15 - 0.5, A.add, *deps)
 
-    def parts(h):
-        ts(T["lb%d" % h][:, 0:32], T["z%d" % h][:], 6, A.logical_shift_right, 255, A.bitwise_and)
-        return ts(T["lb%d" % h][:, 32:64], T["z%d" % h][:], 10, A.logical_shift_right, 0x1F00, A.bitwise_and)
+    def parts(h, *deps):
+        return ts(T["lb%d" % h][:], T["z%d" % h][:], 6, A.logical_shift_right, 0x30FF, A.bitwise_and, *deps)
 
-    def list_w(h, b):
-        return tt(T["ub%d" % h][:], T["lb%d" % h][:, 0:32], T["lb%d" % h][:, 32:64], A.add, b)
+    def list_w(h, t, *deps):
+        return tt(T["ub%d" % h][:], T["lb%d" % h][:], T.cw[:, 32 * t:32 * t + 32], A.add, *deps)
 
-    def list_q(h):
-        return ts(T["la%d" % h][:], T["z%d" % h][:], 63, A.bitwise_and, None, None)
+    def list_q(h, *deps):
+        return ts(T["la%d" % h][:], T["z%d" % h][:], 63, A.bitwise_and, None, None, *deps)
 
     def list0(h, l):
         return activ(T["ua%d" % h][:], T["la%d" % h][:], F.Copy, [l])
 
-    def mask0(h, u):
-        return activ(T["r0%d" % h][:], T.M0[:].indirect(T["ua%d" % h][:]), F.Copy, [u])
+    def mask0(h, u, *deps):
+        return activ(T["r0%d" % h][:], T.M0[:].indirect(T["ua%d" % h][:]), F.Copy, [u] + list(deps))
 
     def mask1(h, m, *deps):
         return activ(T["r1%d" % h][:], T.M1[:, 0:257].indirect(T["um%d" % h][:]), F.Copy, [m] + list(deps))
 
-    constants_1()
-    dK = constants_3()
+    zr = [tt(T["z%d" % h][:], T.st4[:, 32 * h:32 * h + 32], T.cz[:], A.add, dK) for h in range(2)]
+    fill(T.V[:, 16384:16392], 9)
+    la = [list_q(h, zr[h]) for h in range(2)]
+    u = [list0(h, la[h]) for h in range(2)]
+    mk = [[mask0(h, u[h], d0), None] for h in range(2)]
+    um = [rows(h) for h in range(2)]
+    pb = [parts(h) for h in range(2)]
+    d = tt(tc[:, 32:34], tc[:, 22:24], tc[:, 30:32], A.add, f)
+    for i, col in enumerate([20, 26, 28]):
+        for par in range(2):
+            ts(T["dm%d" % (2 * i + par)][:], T.Ih[:], k1(tc, col + par), A.mult, None, None)
+    lb = [list_w(h, 0, pb[h], dC) for h in range(2)]
+    ts(T.adj[:], T.xf[:, 0:4], 3.0, A.is_equal, -2048.0, A.mult)
+    ts(mine[:, 0:772:257], T.xi[:, 0:4], 0.0, A.mult, -2048.0, A.add)
+    ts(T.kt[:], T.xi[:, 0:256], 16.0, A.mult, -8192.0, A.add)
+    for par in range(2):
+        end = 257 if par == 0 else 256
+        ts(T.km[:, par:end:2], T.km[:, par:end:2], k1(tc, 32 + par), A.add, None, None, d)
+
     ld = [("gx0", 16), ("gx1", 16)]
 
-    def pack(h, bank):
+    def pack(h, bank, qs):
         sl = slice(64 * h, 64 * h + 64)
-        return mms([(T[bank][:, 0:256], T.E[sl, 15 - q:143 - q], T.Xb[sl, q:4096:16], q == 0, q == 15) for q in range(16)], [dE, ld[h]])
+        return mms([(T[bank][:, 0:256], T.E[sl, 15 - q:143 - q], T.Xb[sl, q:4096:16], q == 0, q == 15) for q in qs], [dE, ld[h]])
 
-    pkd = [pack(0, "psw")]
+    pkd = [pack(0, "psw", range(16)), None]
     for j in range(4):
         sl = slice(1024 * j, 1024 * (j + 1))
         e = activ(T.Xe[:, sl], T.Xb[:, sl], F.Exp, ld, scale=-math.log(64.0))
+        if j < 2:
+            pkd[1] = pack(1, "pa", range(8 * j, 8 * j + 8))
         hd = mms([(T.psh[:, 64 * j:64 * j + 64], T.Pm[:], T.Xe[:, 1024 * j + q:1024 * (j + 1):16], q == 0, q == 15) for q in range(16)], [dP, e])
-    pkd.append(pack(1, "pa"))
-    dq = []
-    for c in range(3):
-        dq.append(activ(T["q%d" % c][:], T.psh[:, 0:256], F.Copy, [hd], scale=64.0 ** c, bias=BIG))
-        if c < 2:
-            activ(T["e%d" % (c + 1)][:], T["q%d" % c][:], F.Copy, [dq[c]], scale=-64.0, bias=63 * BIG)
+
+    def digits(c):
+        return affine(T["q%d" % c][:], T.psh[:, 0:256], 64.0 ** c, BIG, hd)
+
+    def before(c, d):
+        return affine(T["e%d" % c][:], T["q%d" % (c - 1)][:], -64.0, 63 * BIG, d)
+
+    dq = [digits(0), digits(1)]
+    a = before(1, dq[0])
+    digits(2)
+    dq = [dq[0], a, before(2, dq[1])]
 
     ne = len(topo.engines(core, peers[0]))
 
+    helper, sent = helper_of(core, T, topo), []
+
     def send(ap, sem, deps):
         waits(g, "gq", deps)
-        ids = [DstId(rid=topo.addr(p)[0], pnc=topo.addr(p)[1]) for p in peers]
-        g.remote_dma_fused([RemoteDMATransfer(dst_ids=ids, dma_engine_mask=topo.mask(core, peers[0]), remote_sem=S[sem], srcs=[ap], dsts=[ap for _ in peers])], local_sem=S.ls)
+        sent.append(write(g, T, topo, peers, topo.mask(core, peers[0]), ap, sem))
 
-    def words(b, r, h):
-        return T[b][:, 256 * h:256 * h + 256] if b != "wi" else T.wi[:, 512 * r + 256 * h:512 * r + 256 * h + 256]
+    def hand(i, deps):
+        waits(g, "gq", deps)
+        sent.append(write(g, T, topo, [helper], inner_mask(core, helper, peers[0], topo), handed(T, rank)[i][0], "hin%d" % i))
 
     def letter(r, h, k):
         o = 4096 * r + 2048 * h + 256 * k
         return T.V[:, o:o + 256]
 
-    def unpack(r, h, k, dep):
-        ts(letter(r, h, k), words("wi", r, h), 2 * k, A.logical_shift_right, 3, A.bitwise_and, dep)
+    def unpack(r, h, k):
+        ts(letter(r, h, k), words(T, r, h), 2 * k, A.logical_shift_right, 3, A.bitwise_and, at[r, h])
 
-    def top(r, h, *deps):
-        return activ(letter(r, h, 7), words("vl%d" % r, r, h), F.Copy, deps, scale=2.0 ** -14, bias=2.0 ** -15 - 0.5)
+    def top(part):
+        for r, h in part:
+            e = affine(letter(r, h, 7), words(T, r, h), 2.0 ** -14, 2.0 ** -15 - 0.5, at[r, h])
+        return e
 
     def count(r, c):
         return T["wl%d" % r][:, 257 * c:257 * c + 256]
@@ -256,70 +308,65 @@ def rank_program(g, core, T, topo):
     def left(r, bank, deps):
         return mms([(T[bank][:, 0:256], T.Ih[:], T.kt[:], True, False)] + [(T[bank][:, 0:256], T.In[:], count(r, c), False, c == 2) for c in range(3)], deps)
 
-    def store(r, bank, m, *deps):
-        for c in range(4):
-            e = activ(T.W[:, 1024 * c + 256 * r:1024 * c + 256 * r + 256], count(r, c) if c < 3 else T[bank][:, 0:256], F.Copy, deps if c < 3 else [m])
+    def cols(r, c):
+        return T.W[:, 4096 * r + 256 * c:4096 * r + 256 * c + 256]
+
+    def store(r, cs, bank, m, dep):
+        for c in cs:
+            e = activ(cols(r, c), count(r, c) if c < 3 else T[bank][:, 0:256], F.Copy, [dep if c < 3 else m])
         return e
 
-    zr = [tt(T["z%d" % h][:], T.st4[:, 32 * h:32 * h + 32], T.cz[:], A.add, dK) for h in range(2)]
-    um = [rows(h, zr[h]) for h in range(2)]
-    pb = [parts(h) for h in range(2)]
-    la = [list_q(h) for h in range(2)]
-    lb = [list_w(h, pb[h]) for h in range(2)]
-    constants_0()
-    constants_2()
-
-    own, cw = [], []
-
-    def letters(h, bank, n):
-        vl = words("vl%d" % rank, rank, h)
-        cw.append(copy(vl, T[bank][:, 0:256], pkd[h]))
-        send(vl, "v%d%d" % (rank, h), [cw[h]])
-        own.append(copy(words("wi", rank, h), T[bank][:, 0:256]))
-        for k in range(n):
-            unpack(rank, h, k, own[h])
-
     order = [(rank + NR - k) % NR for k in range(1, NR)]
-    jobs = [(r, h, k) for h in range(2) for r in order for k in range(7)]
-    at = {}
+    come = [(r, h) for h in range(2) for r in order]
+    pairs = [come[0:3], come[3:4], come[4:6]]
+    jobs = [(rank, h, k) for h in range(2) for k in range(8)] + [(r, h, k) for r, h in come for k in range(7)]
+    at = {(r, h): ("v%d%d" % (r, h), ne) for r in order for h in range(2)}
 
     def work(n):
         for r, h, k in jobs[:n]:
-            unpack(r, h, k, at[r, h])
+            unpack(r, h, k)
         del jobs[:n]
 
-    def landed(r, h):
-        at[r, h] = activ(words("wi", r, h), words("vl%d" % r, r, h), F.Copy, [("v%d%d" % (r, h), ne)])
-
-    letters(0, "psw", 8)
+    for h, bank in enumerate(("psw", "pa")):
+        at[rank, h] = copy(words(T, rank, h), T[bank][:, 0:256], pkd[h])
+        if h == 0:
+            send(words(T, rank, h), "v%d0" % rank, [at[rank, h]])
+        else:
+            hand(0, [at[rank, h]])
+            blank(5632, 6912)
+        work(8 - 2 * h)
     for c in range(3):
         s = scan(mine[:, 257 * c + 1:257 * c + 257], T["q%d" % c][:], T["e%d" % c][:], -2048.0, dq[c])
-    to = ts(T["to%d" % rank][:, 0:3], mine[:, 256:771:257], 2048.0, A.add, None, None, s)
+        if c < 2:
+            work(1)
+    ts(T["to%d" % rank][:, 0:3], mine[:, 256:771:257], 2048.0, A.add, None, None, s)
+    to = op(vec, "sv", vec.tensor_reduce, (T["to%d" % rank][:, 3:4], mine[:, 256:771:257], AX.X, A.add), [], {"negate": True})
     send(T["to%d" % rank][:], "t%d" % rank, [to])
-    u = [list0(h, la[h]) for h in range(2)]
-    mk = [[mask0(h, u[h]), None] for h in range(2)]
-    landed(order[0], 0)
-    letters(1, "pa", 7)
-    send(mine[:], "w%d" % rank, [s])
+    hand(1, [s])
+    send(mine[:, 0:CUT], "w%d" % rank, [s])
+    blank(6912, 8192)
+    dG = blank(9216, 12288)
 
-    landed(order[1], 0)
-    landed(order[2], 0)
-    top(rank, 1, cw[1])
-    m0 = left(rank, "psw", [s, own[0]])
-    store(rank, "psw", m0, s)
-    for r in order:
-        top(r, 0, at[r, 0])
+    m0 = left(rank, "psw", [s, at[rank, 0]])
+    store(rank, range(4), "psw", m0, s)
+    top(pairs[0])
 
-    work(6)
-    copy(T.rt[:, rank:12:4], T["to%d" % rank][:, 0:3], to)
+    banks = dict(zip(order, ("psh", "pa", "pb")))
+    wl = {r: ("w%d" % r, ne) for r in order}
+    lf = {}
+
+    def rest(r):
+        lf[r] = left(r, banks[r], [wl[r], ("x%d" % r, ne), at[rank, 1], dq[2]])
+
+    def put(r, cs):
+        for c in cs:
+            e = store(r, [c], banks[r], lf.get(r), wl[r] if c < 2 else ("x%d" % r, ne))
+        return e
+
+    work(11)
+    tt(T.rt[:, rank:16:4], T["to%d" % rank][:], T.adj[:], A.add, to)
     for r in order:
-        a = copy(T.rt[:, r:12:4], T["to%d" % r][:, 0:3], ("t%d" % r, ne))
-    work(1)
-    a = tt(T.tq[:, 0:4], T.rt[:, 0:4], T.rt[:, 4:8], A.add, a)
-    work(1)
-    a = tt(T.tq[:, 4:8], T.tq[:, 0:4], T.rt[:, 8:12], A.add, a)
-    work(1)
-    a = ts(T.rt[:, 12:16], T.tq[:, 4:8], -1.0, A.mult, 4096.0, A.add, a)
+        a = tt(T.rt[:, r:16:4], T["to%d" % r][:], T.adj[:], A.add, ("t%d" % r, ne))
     work(1)
     a = scan(T.inc[:], T.rt[:], T.zz[:], 131200.0, a)
     work(1)
@@ -328,71 +375,74 @@ def rank_program(g, core, T, topo):
     for k in range(16):
         ba = activ(T.bs[:, 16 * k:16 * k + 16], T.Lt[:], F.Identity, [a], bias=k1(T.exc, k), scale=k1(T.rt, k))
     m = mms([(T.psm[:, 0:257], T.BO[:], T.bs[:, 0:257], True, True)], [b, ba])
-    landed(order[0], 1)
+    put(order[0], [0, 1])
     n = 257
-    a = activ(T.dh[:, 0:n], T.psm[:, 0:n], F.Copy, [m], scale=1.0, bias=2.0 ** -12 - 0.5)
-    work(12)
+    a = affine(T.dh[:, 0:n], T.psm[:, 0:n], 1.0, 2.0 ** -12 - 0.5, m)
+    put(order[1], [0])
+    work(10)
     a = tt(T.dr[:, 0:n], T.psm[:, 0:n], T.dh[:, 0:n], A.subtract, a)
-    landed(order[1], 1)
-    a = activ(T.de[:, 0:n], T.dr[:, 0:n], F.Copy, [a], scale=2048.0, bias=2047.75)
+    top(pairs[1])
+    a = affine(T.de[:, 0:n], T.dr[:, 0:n], 2048.0, 2047.75, a)
     for par in range(2):
         m = mms([(T.psd[:, par:par + 129] if par == 0 else T.psm[:, 0:128], T["dm%d" % (2 * i + par)][:], T[buf][:, par:257:2], i == 0, i == 2) for i, buf in enumerate(("dh", "de", "dr"))], [a])
-    work(4)
+    for r in order:
+        rest(r)
+    put(order[1], [1])
+    put(order[2], [0, 1])
+    dT = top(pairs[2])
+    work(5)
     for par in range(2):
         n, end = 129 - par, 257 if par == 0 else 256
         dM = tt(T.M1[:, par:end:2], (T.psd if par == 0 else T.psm)[:, 0:n], T.km[:, par:end:2], A.add, m)
-    landed(order[2], 1)
-    banks = ("psh", "pa", "pb")
-    lf = [left(r, b, [("w%d" % r, ne), own[1], dq[2]]) for r, b in zip(order, banks)]
-    for i, r in enumerate(order):
-        dT = top(r, 1, at[r, 1])
-        if i == 2:
-            mk[0][1] = mask1(0, um[0], dM)
-        dW = store(r, banks[i], lf[i], ("w%d" % r, ne))
+    for r in order:
+        dW = put(r, [2, 3])
+    mk[0][1] = mask1(0, um[0], dM)
     mk[1][1] = mask1(1, um[1], dM)
     work(len(jobs))
     dV = ("sv", cnt["sv"])
 
     res, du = [None, None], [dT, dT]
 
-    def sums(h, y, first, deps):
-        items = [(T["ps%d" % h][:, 0:32], T.ES[:, 15 - q:143 - q], T[y][:, q::16], first and q == 0, (not first) and q == 15) for q in range(16)]
+    def sums(h, y, nxt, deps):
+        ps = T["ps%d" % h][:, 0:32]
+        items = [(ps, T.ES[:, 15 - q:143 - q], T[y][:, q::16], nxt is not None and q == 0, nxt is None and q == 15) for q in range(16)]
+        if nxt is not None and nxt < ST:
+            items.append((ps, T.Ih[:], T.cq[:, 32 * nxt:32 * nxt + 32], False, False))
         return mms(items, deps)
 
-    def y1(h, first):
+    def y1(h, nxt=None):
         e = tt(T["ya%d" % h][:], T.V[:].indirect(T["uv%d" % h][:]), T["r0%d" % h][:], A.is_equal, du[h], mk[h][0], dV)
-        return sums(h, "ya%d" % h, first, [e])
+        return sums(h, "ya%d" % h, nxt, [e])
 
-    def y2(h, first):
-        e = tt(T["yb%d" % h][:], T.W[:, 0:4097].indirect(T["ub%d" % h][:]), T["r1%d" % h][:], A.max, lb[h], mk[h][1], dW)
-        return sums(h, "yb%d" % h, first, [e, du[h]])
+    def y2(h, nxt=None):
+        e = tt(T["yb%d" % h][:], T.W[:].indirect(T["ub%d" % h][:]), T["r1%d" % h][:], A.max, lb[h], mk[h][1], dW, dG)
+        return sums(h, "yb%d" % h, nxt, [e, du[h]])
 
     def head(h, t):
-        z = tt(T["z%d" % h][:], T["ps%d" % h][:, 0:32], T.cl[:, 32 * t:32 * t + 32], A.add, res[h])
-        mk[h][1] = mask1(h, rows(h, z))
+        ps = T["ps%d" % h][:, 0:32]
+        z = ts(T["z%d" % h][:], ps, 2.0 ** 14, A.mult, -4.0 * KC, A.add, res[h])
+        m = tt(T["um%d" % h][:], ps, T.cm[:, 32 * t:32 * t + 32], A.add)
+        mk[h][1] = mask1(h, m)
+        b = parts(h, z)
         u = list0(h, list_q(h))
-        du[h] = activ(T["uv%d" % h][:], T["ps%d" % h][:, 0:32], F.Copy, [res[h]], scale=1.0 / 64, bias=-KC / 16.0 - 15.0 / 32)
+        lb[h] = list_w(h, t, b)
+        du[h] = affine(T["uv%d" % h][:], ps, 256.0, 2.0 ** -7 - 0.5 - KC / 16.0)
         mk[h][0] = mask0(h, u)
 
-    def tail(h):
-        lb[h] = list_w(h, parts(h))
-
-    y1(0, True)
-    res[0] = y2(0, False)
-    y2(1, True)
+    y1(0, 1)
+    res[0] = y2(0)
+    y2(1, 1)
     for t in range(1, ST):
         head(0, t)
-        res[1] = y1(1, False)
-        tail(0)
-        y2(0, True)
+        res[1] = y1(1)
+        y2(0, t + 1)
         head(1, t)
-        res[0] = y1(0, False)
-        tail(1)
-        y2(1, True)
-    res[1] = y1(1, False)
+        res[0] = y1(0)
+        y2(1, t + 1)
+    res[1] = y1(1)
     for h in range(2):
-        e = ts(T["yo%d" % h][:], T["ps%d" % h][:, 0:32], 0.25, A.mult, -float(KC), A.add, res[h])
+        e = ts(T["yo%d" % h][:], T["ps%d" % h][:, 0:32], 4096.0, A.mult, -float(KC), A.add, res[h])
         waits(syn, "sy", [e])
         syn.dma_start(T.y[:, 32 * h:32 * h + 32], T["yo%d" % h][:]).then_inc(S["yd%d" % h], 16)
     waits(syn, "sy", [("yd0", 16), ("yd1", 16)])
-    g.wait_ge(S.ls, 4 * ne)
+    g.wait_ge(S.ls, sum(sent))

@@ -8,16 +8,17 @@ KC = 30718 - 2048
 BIG = 12582912.0
 SCRATCH = {
     "Xb": ("sbuf", [128, 4096], "bfloat16"), "Xe": ("sbuf", [128, 4096], "bfloat16"),
-    "V": ("sbuf", [128, 16392], "int32"), "W": ("sbuf", [128, 13312], "int32"), "cw": ("sbuf", [128, 256], "int32"),
-    "q0": ("sbuf", [128, 256], "float32"), "q1": ("sbuf", [128, 256], "float32"), "q2": ("sbuf", [128, 256], "float32"),
-    "e0": ("sbuf", [128, 256], "float32"), "e1": ("sbuf", [128, 256], "float32"), "e2": ("sbuf", [128, 256], "float32"),
+    "V": ("sbuf", [128, 16392], "int32"), "W": ("sbuf", [128, 13312], "float32"), "wi": ("sbuf", [128, 2048], "int32"),
+    "vl": ("sbuf", [128, 1024], "uint16"),
+    "q0": ("sbuf", [128, 256], "uint16"), "q1": ("sbuf", [128, 256], "uint16"), "q2": ("sbuf", [128, 256], "uint16"),
+    "e0": ("sbuf", [128, 256], "uint16"), "e1": ("sbuf", [128, 256], "uint16"), "e2": ("sbuf", [128, 256], "uint16"),
     "zz": ("sbuf", [128, 16], "float32"), "kt": ("sbuf", [128, 256], "float16"),
     "rt": ("sbuf", [128, 16], "float32"), "inc": ("sbuf", [128, 16], "float32"), "exc": ("sbuf", [128, 16], "float32"),
     "adj": ("sbuf", [128, 4], "float32"),
     "bs": ("sbuf", [128, 264], "float32"),
     "dh": ("sbuf", [128, 264], "float16"), "dr": ("sbuf", [128, 264], "float16"), "de": ("sbuf", [128, 264], "float16"),
     "M1": ("sbuf", [128, 264], "float32"),
-    "M0": ("sbuf", [128, 64], "bfloat16"), "km": ("sbuf", [128, 264], "float32"), "jq": ("sbuf", [128, 264], "int32"),
+    "M0": ("sbuf", [128, 64], "bfloat16"), "km": ("sbuf", [128, 528], "bfloat16"), "jq": ("sbuf", [128, 264], "int32"),
     "xi": ("sbuf", [128, 264], "int32"), "xf": ("sbuf", [128, 264], "float32"), "pi": ("sbuf", [128, 1], "int32"),
     "pk": ("sbuf", [128, 8], "int32"), "pf": ("sbuf", [128, 8], "float32"), "tc": ("sbuf", [128, 40], "float32"),
     "w4": ("sbuf", [128, 1], "float32"),
@@ -26,7 +27,7 @@ SCRATCH = {
     "xg": ("sbuf", [128, 128], "int32"), "BO": ("sbuf", [128, 128], "float32"),
     "Lt": ("sbuf", [128, 16], "float32"), "m0i": ("sbuf", [128, 128], "int32"), "m0f": ("sbuf", [128, 128], "float32"),
     "pats_s": ("sbuf", [128, 256], "int32"), "st_s": ("sbuf", [128, 64], "int32"), "cm": ("sbuf", [128, 256], "float32"),
-    "cq": ("sbuf", [128, 256], "float16"),
+    "cw": ("sbuf", [128, 256], "float32"), "cq": ("sbuf", [128, 256], "float16"), "kd": ("sbuf", [128, 264], "float16"),
     "cz": ("sbuf", [128, 32], "int32"), "st4": ("sbuf", [128, 64], "int32"),
     "psw": ("psum", [128, 512], "float32"), "psh": ("psum", [128, 512], "float32"), "psm": ("psum", [128, 512], "float32"),
     "psd": ("psum", [128, 512], "float32"), "pa": ("psum", [128, 512], "float32"), "pb": ("psum", [128, 512], "float32"),
@@ -51,8 +52,8 @@ for _h in range(2):
     SCRATCH["yb%d" % _h] = ("sbuf", [128, 512], "float16")
     SCRATCH["yo%d" % _h] = ("sbuf", [128, 32], "float32")
 SEMAPHORES = ["sv", "sa", "st", "sg", "ls", "gx0", "gx1", "ldp", "yd0", "yd1"] + ["%s%d" % (s, k) for s in "wt" for k in range(NR)] + ["v%d%d" % (k, h) for k in range(NR) for h in range(2)]
-SEMAPHORES += ["hin0", "hin1"] + ["x%d" % k for k in range(NR)]
-CUT = 514
+SEMAPHORES += ["hin0", "hin1"] + ["%s%d" % (s, k) for s in "xu" for k in range(NR)]
+CUT = 257
 
 
 def helper_of(core, T, topo):
@@ -65,16 +66,21 @@ def write(g, T, topo, cores, mask, ap, sem):
     return bin(mask).count("1")
 
 
-def words(T, r, h):
-    return T.W[:, 1024 + 512 * r + 256 * h:1280 + 512 * r + 256 * h]
+def words(T, r, h, j=None):
+    o = 512 * r + 256 * h
+    return T.wi[:, o:o + 256] if j is None else T.wi[:, o + 128 * j:o + 128 * j + 128]
+
+
+def short(T, r):
+    return [T.vl[:, 256 * r:256 * r + 128], T.vl[:, 256 * r + 128:256 * r + 256], T.vl[:, 256 * r:256 * r + 256]]
 
 
 def handed(T, rank):
-    return [(words(T, rank, 1), "v%d1" % rank), (T["wl%d" % rank][:, CUT:772], "x%d" % rank)]
+    return [(short(T, rank)[2], "v%d1" % rank), (T["wl%d" % rank][:, 0:CUT], "x%d" % rank)]
 
 
 def inner_mask(core, helper, peer, topo):
-    return topo.mask(core, helper) & ~topo.mask(core, peer)
+    return sum(1 << e for e in [e for e in topo.engines(core, helper) if e not in topo.engines(core, peer)][::2])
 
 
 def hand_on(g, core, T, topo):
@@ -125,7 +131,7 @@ def rank_program(g, core, T, topo):
         return op(vec, "sv", vec.memset, (ap, v), deps)
 
     def scan(out, a, b, i, *deps):
-        return op(vec, "sv", vec.tensor_tensor_scan, (out, a, b, i, A.add, A.add), deps)
+        return op(vec, "sv", vec.tensor_tensor_scan, (out, a, b, i, A.add, A.subtract), deps)
 
     def activ(out, in_, f, deps, **kw):
         return op(act, "sa", act.activation, (out, in_, f), deps, kw)
@@ -145,12 +151,7 @@ def rank_program(g, core, T, topo):
     op(g, "sg", g.iota, (T.pi[:], [[1, 1]], 0, 1), [])
     for h in range(2):
         g.dma_start(T.Xb[64 * h:64 * h + 64, :], T.bwt[:, 32768 * h:32768 * h + 32768]).then_inc(S["gx%d" % h], 16)
-
-    def blank(a, b):
-        return op(g, "sg", g.iota, (T.W[:, a:b], [[0, b - a]], 0, 0), [])
-
-    blank(3072, 4096)
-    blank(5120, 5632)
+    op(g, "sg", g.iota, (T.V[:, 16384:16392], [[0, 8]], 9, 0), [])
     syn.dma_start(T.pats_s[:], T.pats[:]).then_inc(S.ldp, 16)
     syn.dma_start(T.st_s[:], T.starts[:]).then_inc(S.ldp, 16)
 
@@ -160,10 +161,11 @@ def rank_program(g, core, T, topo):
     def k1(b, i):
         return b[:, i:i + 1]
 
-    a = fill(T.km[:], 0.5)
+    fill(T.km[:, 0:264], 1.0)
+    a = fill(T.km[:, 264:528], 0.0)
     for i, (sh, mk) in enumerate([(0, 1), (0, 7), (0, 56), (3, 1), (0, 15), (0, 112), (0, 127), (0, 64)]):
         d = ts(k1(pk, i), T.pi[:], sh, A.logical_shift_right, mk, A.bitwise_and, ("sg", 1))
-    dx = scan(T.xf[:], T.km[:], T.km[:], -1.0, a)
+    dx = scan(T.xf[:], T.km[:, 0:264], T.km[:, 264:528], -1.0, a)
     dp = copy(pf[:, 0:8], pk[:, 0:8], d)
     dw = activ(T.w4[:], k1(pf, 1), F.Exp, [dp], scale=math.log(4.0))
     di = copy(T.xi[:], T.xf[:], dx)
@@ -186,36 +188,6 @@ def rank_program(g, core, T, topo):
     d0 = ts(T.M0[:], T.m0f[:, 0:64], -1.0, A.add, None, None, a)
     dE = ts(T.E[:], T.xf[:, 0:144], k1(tc, 3), A.is_equal, T.w4[:], A.mult, dw)
 
-    affine(T.st4[:], T.st_s[:], 4.0, 0.0, ("ldp", 32))
-    dK = affine(T.cz[:], T.pats_s[:, 0:32], 1048577.0, 0.0)
-    for h in range(2):
-        affine(T["uv%d" % h][:], T.st_s[:, 32 * h:32 * h + 32], 1.0 / 16, -15.0 / 32)
-    affine(T.cm[:], T.pats_s[:], 64.0, 2.0 ** -15 - 0.5 - KC / 4096.0)
-    affine(T.cq[:], T.pats_s[:], 2.0 ** -14, 0.0)
-    dC = affine(T.cw[:], T.pats_s[:], 256.0, 0.0)
-    affine(T.e0[:], T.xf[:, 0:256], 0.0, -BIG, dx)
-    affine(T.In[:], T.Ih[:], -1.0, 0.0, dI)
-
-    ts(k1(tc, 8), k1(pf, 3), -448.0, A.mult, 448.0, A.add)
-    for i, v in enumerate([9, 8]):
-        ts(k1(tc, 10 + i), k1(pf, 4), float(v), A.is_equal, 256.0, A.mult)
-    for i, v in enumerate([11, 10, 13, 12]):
-        a = ts(k1(tc, 12 + i), k1(pf, 4), float(v), A.is_equal, None, None)
-    ts(T.km[:], T.jq[:], k1(pf, 4), A.is_equal, -6144.0, A.mult, d0)
-    b = tt(k1(tc, 18), k1(tc, 8), k1(pf, 0), A.mult, a)
-    c = ts(tc[:, 22:24], tc[:, 12:14], -2048.0, A.mult, 2048.0, A.add)
-    d = ts(tc[:, 24:26], tc[:, 14:16], 2046.0, A.mult, None, None)
-    b = tt(k1(tc, 19), k1(tc, 8), k1(tc, 18), A.subtract, b)
-    tt(tc[:, 26:28], tc[:, 12:14], tc[:, 14:16], A.subtract)
-    ts(tc[:, 28:30], tc[:, 14:16], 2048.0, A.mult, None, None)
-    b = tt(tc[:, 20:22], tc[:, 18:20], tc[:, 10:12], A.add, b)
-    d = tt(tc[:, 22:24], tc[:, 22:24], tc[:, 24:26], A.add, d)
-    fill(T.zz[:], 0.0)
-    f = ts(tc[:, 30:32], tc[:, 20:22], -1025.0, A.mult, None, None, b)
-
-    def rows(h, *deps):
-        return ts(T["um%d" % h][:], T["z%d" % h][:], 2.0 ** -14, A.mult, 2.0 ** -15 - 0.5, A.add, *deps)
-
     def parts(h, *deps):
         return ts(T["lb%d" % h][:], T["z%d" % h][:], 6, A.logical_shift_right, 0x30FF, A.bitwise_and, *deps)
 
@@ -234,49 +206,63 @@ def rank_program(g, core, T, topo):
     def mask1(h, m, *deps):
         return activ(T["r1%d" % h][:], T.M1[:, 0:257].indirect(T["um%d" % h][:]), F.Copy, [m] + list(deps))
 
+    affine(T.st4[:], T.st_s[:], 4.0, 0.0, ("ldp", 32))
+    dK = affine(T.cz[:], T.pats_s[:, 0:32], 1048577.0, 0.0)
+    for h in range(2):
+        affine(T["uv%d" % h][:], T.st_s[:, 32 * h:32 * h + 32], 1.0 / 16, -15.0 / 32)
+    affine(T.cq[:], T.pats_s[:], 2.0 ** -14, 0.0)
     zr = [tt(T["z%d" % h][:], T.st4[:, 32 * h:32 * h + 32], T.cz[:], A.add, dK) for h in range(2)]
-    fill(T.V[:, 16384:16392], 9)
+    dC = ts(T.cw[:], T.pats_s[:], 256.0, A.mult, None, None)
     la = [list_q(h, zr[h]) for h in range(2)]
-    u = [list0(h, la[h]) for h in range(2)]
-    mk = [[mask0(h, u[h], d0), None] for h in range(2)]
-    um = [rows(h) for h in range(2)]
     pb = [parts(h) for h in range(2)]
-    d = tt(tc[:, 32:34], tc[:, 22:24], tc[:, 30:32], A.add, f)
-    for i, col in enumerate([20, 26, 28]):
-        for par in range(2):
-            ts(T["dm%d" % (2 * i + par)][:], T.Ih[:], k1(tc, col + par), A.mult, None, None)
+    u = [list0(h, la[h]) for h in range(2)]
+    um = [affine(T["um%d" % h][:], T["z%d" % h][:], 2.0 ** -14, 2.0 ** -15 - 0.5) for h in range(2)]
+    mk = [[mask0(0, u[0], d0), None], [None, None]]
+    ts(T.In[:], T.Ih[:], -1.0, A.mult, None, None)
+    fill(T.e0[:], 0)
     lb = [list_w(h, 0, pb[h], dC) for h in range(2)]
-    ts(T.adj[:], T.xf[:, 0:4], 3.0, A.is_equal, -2048.0, A.mult)
+
+    ts(k1(tc, 8), k1(pf, 3), -448.0, A.mult, 448.0, A.add)
+    for i, v in enumerate([9, 8]):
+        ts(k1(tc, 10 + i), k1(pf, 4), float(v), A.is_equal, 256.0, A.mult)
+    for i, v in enumerate([11, 10, 13, 12]):
+        a = ts(k1(tc, 12 + i), k1(pf, 4), float(v), A.is_equal, None, None)
+    ts(T.kd[:], T.jq[:], k1(pf, 4), A.is_equal, -6144.0, A.mult, d0)
+    b = tt(k1(tc, 18), k1(tc, 8), k1(pf, 0), A.mult, a)
+    c = ts(tc[:, 22:24], tc[:, 12:14], -2048.0, A.mult, 2048.0, A.add)
+    d = ts(tc[:, 24:26], tc[:, 14:16], 2046.0, A.mult, None, None)
+    b = tt(k1(tc, 19), k1(tc, 8), k1(tc, 18), A.subtract, b)
+    tt(tc[:, 26:28], tc[:, 12:14], tc[:, 14:16], A.subtract)
+    ts(tc[:, 28:30], tc[:, 14:16], 2048.0, A.mult, None, None)
+    b = tt(tc[:, 20:22], tc[:, 18:20], tc[:, 10:12], A.add, b)
+    d = tt(tc[:, 22:24], tc[:, 22:24], tc[:, 24:26], A.add, d)
+    fill(T.zz[:], 0.0)
+    f = ts(tc[:, 30:32], tc[:, 20:22], -1025.0, A.mult, None, None, b)
     ts(mine[:, 0:772:257], T.xi[:, 0:4], 0.0, A.mult, -2048.0, A.add)
-    ts(T.kt[:], T.xi[:, 0:256], 16.0, A.mult, -8192.0, A.add)
-    for par in range(2):
-        end = 257 if par == 0 else 256
-        ts(T.km[:, par:end:2], T.km[:, par:end:2], k1(tc, 32 + par), A.add, None, None, d)
+    ts(T.adj[:], T.xf[:, 0:4], 3.0, A.is_equal, -2048.0, A.mult)
+    tt(tc[:, 32:34], tc[:, 22:24], tc[:, 30:32], A.add, f)
+
+    def later():
+        ts(T.kt[:], T.xf[:, 0:256], 16.0, A.mult, -8192.0, A.add)
+        for i, col in enumerate([20, 26, 28]):
+            for par in range(2):
+                ts(T["dm%d" % (2 * i + par)][:], T.Ih[:], k1(tc, col + par), A.mult, None, None)
 
     ld = [("gx0", 16), ("gx1", 16)]
 
-    def pack(h, bank, qs):
+    packs = {(0, 0): "psw", (0, 1): "psd", (1, 0): "pa", (1, 1): "pb"}
+    pkd, at, hd, hist = {}, {}, {}, [T.psh, T.psm]
+    for (h, j), bank in packs.items():
         sl = slice(64 * h, 64 * h + 64)
-        return mms([(T[bank][:, 0:256], T.E[sl, 15 - q:143 - q], T.Xb[sl, q:4096:16], q == 0, q == 15) for q in qs], [dE, ld[h]])
-
-    pkd = [pack(0, "psw", range(16)), None]
+        pkd[h, j] = mms([(T[bank][:, 0:128], T.E[sl, 15 - q:143 - q], T.Xb[sl, 2048 * j + q:2048 * j + 2048:16], q == 0, q == 15) for q in range(16)], [dE, ld[h]])
     for j in range(4):
         sl = slice(1024 * j, 1024 * (j + 1))
-        e = activ(T.Xe[:, sl], T.Xb[:, sl], F.Exp, ld, scale=-math.log(64.0))
-        if j < 2:
-            pkd[1] = pack(1, "pa", range(8 * j, 8 * j + 8))
-        hd = mms([(T.psh[:, 64 * j:64 * j + 64], T.Pm[:], T.Xe[:, 1024 * j + q:1024 * (j + 1):16], q == 0, q == 15) for q in range(16)], [dP, e])
+        e = activ(T.Xe[:, sl], T.Xb[:, sl], F.Exp, ld, scale=-math.log(32.0))
+        hd[j // 2] = mms([(hist[j // 2][:, 64 * (j % 2):64 * (j % 2) + 64], T.Pm[:], T.Xe[:, 1024 * j + q:1024 * (j + 1):16], q == 0, q == 15) for q in range(16)], [dP, e])
 
-    def digits(c):
-        return affine(T["q%d" % c][:], T.psh[:, 0:256], 64.0 ** c, BIG, hd)
-
-    def before(c, d):
-        return affine(T["e%d" % c][:], T["q%d" % (c - 1)][:], -64.0, 63 * BIG, d)
-
-    dq = [digits(0), digits(1)]
-    a = before(1, dq[0])
-    digits(2)
-    dq = [dq[0], a, before(2, dq[1])]
+    dq = [affine(T["q%d" % c][:, 128:256], hist[1][:, 0:128], 32.0 ** c, -1.0 / 64, hd[1]) for c in range(3)]
+    mk[1][0] = mask0(1, u[1])
+    affine(T.cm[:], T.pats_s[:], 64.0, 2.0 ** -15 - 0.5 - KC / 4096.0)
 
     ne = len(topo.engines(core, peers[0]))
 
@@ -290,16 +276,19 @@ def rank_program(g, core, T, topo):
         waits(g, "gq", deps)
         sent.append(write(g, T, topo, [helper], inner_mask(core, helper, peers[0], topo), handed(T, rank)[i][0], "hin%d" % i))
 
-    def letter(r, h, k):
+    def letter(r, h, k, j=None):
         o = 4096 * r + 2048 * h + 256 * k
-        return T.V[:, o:o + 256]
+        return T.V[:, o:o + 256] if j is None else T.V[:, o + 128 * j:o + 128 * j + 128]
 
-    def unpack(r, h, k):
-        ts(letter(r, h, k), words(T, r, h), 2 * k, A.logical_shift_right, 3, A.bitwise_and, at[r, h])
+    def there(r, h, j):
+        return [at[r, h, i] for i in range(2) if j in (i, None)]
+
+    def unpack(r, h, j, k):
+        ts(letter(r, h, k, j), words(T, r, h, j), 2 * k, A.logical_shift_right, 3, A.bitwise_and, *there(r, h, j))
 
     def top(part):
         for r, h in part:
-            e = affine(letter(r, h, 7), words(T, r, h), 2.0 ** -14, 2.0 ** -15 - 0.5, at[r, h])
+            e = affine(letter(r, h, 7), words(T, r, h), 2.0 ** -14, 2.0 ** -15 - 0.5, *there(r, h, None))
         return e
 
     def count(r, c):
@@ -311,59 +300,68 @@ def rank_program(g, core, T, topo):
     def cols(r, c):
         return T.W[:, 4096 * r + 256 * c:4096 * r + 256 * c + 256]
 
-    def store(r, cs, bank, m, dep):
-        for c in cs:
-            e = activ(cols(r, c), count(r, c) if c < 3 else T[bank][:, 0:256], F.Copy, [dep if c < 3 else m])
-        return e
+    def store(r, c, dep):
+        waits(g, "gq", [dep])
+        return op(g, "sg", g.affine_select, (cols(r, c), count(r, c), [[0, 256]], A.is_ge, 0.0, 0, 0), [])
+
+    def last(r, bank, m):
+        return affine(cols(r, 3), T[bank][:, 0:256], 1.0, 0.0, m)
 
     order = [(rank + NR - k) % NR for k in range(1, NR)]
     come = [(r, h) for h in range(2) for r in order]
-    pairs = [come[0:3], come[3:4], come[4:6]]
-    jobs = [(rank, h, k) for h in range(2) for k in range(8)] + [(r, h, k) for r, h in come for k in range(7)]
-    at = {(r, h): ("v%d%d" % (r, h), ne) for r in order for h in range(2)}
+    parts_ = [(r, 0, j) for j in range(2) for r in order[:2]] + [(r, h, None) for r, h in come[2:]]
+    jobs = [(rank, h, j, k) for h in range(2) for j in range(2) for k in range(7)] + [x + (k,) for x in parts_ for k in range(7)]
+    for r in order:
+        at.update({(r, 0, 0): ("u%d" % r, ne), (r, 0, 1): ("v%d0" % r, ne), (r, 1, 0): ("v%d1" % r, ne), (r, 1, 1): ("v%d1" % r, ne)})
+
+    def widen(r):
+        at[r, 1, 0] = at[r, 1, 1] = affine(words(T, r, 1), short(T, r)[2], 1.0, 0.0, ("v%d1" % r, ne))
 
     def work(n):
-        for r, h, k in jobs[:n]:
-            unpack(r, h, k)
+        for job in jobs[:n]:
+            unpack(*job)
         del jobs[:n]
 
-    for h, bank in enumerate(("psw", "pa")):
-        at[rank, h] = copy(words(T, rank, h), T[bank][:, 0:256], pkd[h])
+    for i, ((h, j), bank) in enumerate(packs.items()):
+        at[rank, h, j] = copy(words(T, rank, h, j), T[bank][:, 0:128], pkd[h, j])
         if h == 0:
-            send(words(T, rank, h), "v%d0" % rank, [at[rank, h]])
+            send(words(T, rank, 0, j), ("u%d", "v%d0")[j] % rank, [at[rank, 0, j]])
         else:
-            hand(0, [at[rank, h]])
-            blank(5632, 6912)
-        work(8 - 2 * h)
+            a = copy(short(T, rank)[j], T[bank][:, 0:128])
+        work(6 if i == 0 else 7)
+        if i == 3:
+            hand(0, [a])
+    later()
+    def before(c, j, d):
+        return ts(T["e%d" % c][:, 128 * j:128 * j + 128], T["q%d" % (c - 1)][:, 128 * j:128 * j + 128], 32.0, A.mult, None, None, d)
+
+    a = [ts(T["q%d" % c][:, 0:128], hist[0][:, 0:128], 32.0 ** c, A.mult, -1.0 / 64, A.add, hd[0]) for c in range(3)]
+    b = [before(c, 0, a[c - 1]) for c in (1, 2)][1]
+    work(1 + 6)
     for c in range(3):
-        s = scan(mine[:, 257 * c + 1:257 * c + 257], T["q%d" % c][:], T["e%d" % c][:], -2048.0, dq[c])
-        if c < 2:
-            work(1)
+        e = before(c + 1, 1, dq[c]) if c < 2 else None
+        s = scan(mine[:, 257 * c + 1:257 * c + 257], T["q%d" % c][:], T["e%d" % c][:], -2048.0, dq[c], b)
+        if c == 0:
+            hand(1, [s])
+        b = e
+    work(1)
     ts(T["to%d" % rank][:, 0:3], mine[:, 256:771:257], 2048.0, A.add, None, None, s)
     to = op(vec, "sv", vec.tensor_reduce, (T["to%d" % rank][:, 3:4], mine[:, 256:771:257], AX.X, A.add), [], {"negate": True})
     send(T["to%d" % rank][:], "t%d" % rank, [to])
-    hand(1, [s])
-    send(mine[:, 0:CUT], "w%d" % rank, [s])
-    blank(6912, 8192)
-    dG = blank(9216, 12288)
+    send(mine[:, CUT:772], "w%d" % rank, [s])
+    for c in range(3):
+        store(rank, c, s)
+    for r in order:
+        for c in (1, 2):
+            store(r, c, ("w%d" % r, ne))
+    for r in order[1:]:
+        dG = store(r, 0, ("x%d" % r, ne))
 
-    m0 = left(rank, "psw", [s, at[rank, 0]])
-    store(rank, range(4), "psw", m0, s)
-    top(pairs[0])
+    dL = last(rank, "psw", left(rank, "psw", [s]))
+    top([(rank, 0), (rank, 1)] + come[:3])
 
     banks = dict(zip(order, ("psh", "pa", "pb")))
-    wl = {r: ("w%d" % r, ne) for r in order}
-    lf = {}
-
-    def rest(r):
-        lf[r] = left(r, banks[r], [wl[r], ("x%d" % r, ne), at[rank, 1], dq[2]])
-
-    def put(r, cs):
-        for c in cs:
-            e = store(r, [c], banks[r], lf.get(r), wl[r] if c < 2 else ("x%d" % r, ne))
-        return e
-
-    work(11)
+    work(21 + 2)
     tt(T.rt[:, rank:16:4], T["to%d" % rank][:], T.adj[:], A.add, to)
     for r in order:
         a = tt(T.rt[:, r:16:4], T["to%d" % r][:], T.adj[:], A.add, ("t%d" % r, ne))
@@ -372,31 +370,31 @@ def rank_program(g, core, T, topo):
     work(1)
     b = copy(T.bs[:, 256:257], T.inc[:, 15:16], a)
     a = tt(T.exc[:], T.inc[:], T.rt[:], A.subtract, a)
+    work(1)
     for k in range(16):
-        ba = activ(T.bs[:, 16 * k:16 * k + 16], T.Lt[:], F.Identity, [a], bias=k1(T.exc, k), scale=k1(T.rt, k))
-    m = mms([(T.psm[:, 0:257], T.BO[:], T.bs[:, 0:257], True, True)], [b, ba])
-    put(order[0], [0, 1])
+        ba = ts(T.bs[:, 16 * k:16 * k + 16], T.Lt[:], k1(T.rt, k), A.mult, k1(T.exc, k), A.add, a)
+    widen(order[0])
+    widen(order[1])
     n = 257
+    m = mms([(T.psm[:, 0:n], T.BO[:], T.bs[:, 0:n], True, True)], [b, ba])
+    mms([(T.psd[:, 0:n], T.BO[:], T.bs[:, 0:n], True, False)], [])
     a = affine(T.dh[:, 0:n], T.psm[:, 0:n], 1.0, 2.0 ** -12 - 0.5, m)
-    put(order[1], [0])
-    work(10)
-    a = tt(T.dr[:, 0:n], T.psm[:, 0:n], T.dh[:, 0:n], A.subtract, a)
-    top(pairs[1])
-    a = affine(T.de[:, 0:n], T.dr[:, 0:n], 2048.0, 2047.75, a)
-    for par in range(2):
-        m = mms([(T.psd[:, par:par + 129] if par == 0 else T.psm[:, 0:128], T["dm%d" % (2 * i + par)][:], T[buf][:, par:257:2], i == 0, i == 2) for i, buf in enumerate(("dh", "de", "dr"))], [a])
-    for r in order:
-        rest(r)
-    put(order[1], [1])
-    put(order[2], [0, 1])
-    dT = top(pairs[2])
-    work(5)
-    for par in range(2):
-        n, end = 129 - par, 257 if par == 0 else 256
-        dM = tt(T.M1[:, par:end:2], (T.psd if par == 0 else T.psm)[:, 0:n], T.km[:, par:end:2], A.add, m)
-    for r in order:
-        dW = put(r, [2, 3])
+    m = mms([(T.psd[:, 0:n], T.In[:], T.dh[:, 0:n], False, True)], [a])
+    widen(order[2])
+    affine(T.dr[:, 0:n], T.psd[:, 0:n], 1.0, 0.0, m)
+    a = affine(T.de[:, 0:n], T.psd[:, 0:n], 2048.0, 2047.75)
+    side = [(T.psm[:, 0:129], slice(0, 257, 2)), (T.psw[:, 0:128], slice(1, 256, 2))]
+    mp = [mms([(ps, T["dm%d" % (2 * i + par)][:], T[buf][:, sl], i == 0, False) for i, buf in enumerate(("dh", "de", "dr"))] + [(ps, T.Ih[:], T.kd[:, sl], False, True)], [a, dL]) for par, (ps, sl) in enumerate(side)]
+    lf = [left(r, banks[r], [("w%d" % r, ne), ("x%d" % r, ne), dq[2]]) for r in order]
+    top(come[3:5])
+    for par, (ps, sl) in enumerate(side):
+        dM = activ(T.M1[:, sl], ps, F.Identity, [mp[par]], bias=k1(tc, 32 + par))
+    dT = top(come[5:6])
     mk[0][1] = mask1(0, um[0], dM)
+    for i, r in enumerate(order):
+        if i < 1:
+            affine(cols(r, 0), count(r, 0), 1.0, 0.0, ("x%d" % r, ne))
+        dW = last(r, banks[r], lf[i])
     mk[1][1] = mask1(1, um[1], dM)
     work(len(jobs))
     dV = ("sv", cnt["sv"])
@@ -411,7 +409,7 @@ def rank_program(g, core, T, topo):
         return mms(items, deps)
 
     def y1(h, nxt=None):
-        e = tt(T["ya%d" % h][:], T.V[:].indirect(T["uv%d" % h][:]), T["r0%d" % h][:], A.is_equal, du[h], mk[h][0], dV)
+        e = tt(T["ya%d" % h][:], T.V[:].indirect(T["uv%d" % h][:]), T["r0%d" % h][:], A.is_equal, du[h], mk[h][0], dV, ("sg", 2))
         return sums(h, "ya%d" % h, nxt, [e])
 
     def y2(h, nxt=None):
@@ -421,24 +419,21 @@ def rank_program(g, core, T, topo):
     def head(h, t):
         ps = T["ps%d" % h][:, 0:32]
         z = ts(T["z%d" % h][:], ps, 2.0 ** 14, A.mult, -4.0 * KC, A.add, res[h])
-        m = tt(T["um%d" % h][:], ps, T.cm[:, 32 * t:32 * t + 32], A.add)
-        mk[h][1] = mask1(h, m)
+        mk[h][1] = mask1(h, tt(T["um%d" % h][:], ps, T.cm[:, 32 * t:32 * t + 32], A.add))
         b = parts(h, z)
         u = list0(h, list_q(h))
-        lb[h] = list_w(h, t, b)
         du[h] = affine(T["uv%d" % h][:], ps, 256.0, 2.0 ** -7 - 0.5 - KC / 16.0)
         mk[h][0] = mask0(h, u)
+        res[1 - h] = y1(1 - h)
+        lb[h] = list_w(h, t, b)
+        y2(h, t + 1)
 
     y1(0, 1)
     res[0] = y2(0)
     y2(1, 1)
     for t in range(1, ST):
         head(0, t)
-        res[1] = y1(1)
-        y2(0, t + 1)
         head(1, t)
-        res[0] = y1(0)
-        y2(1, t + 1)
     res[1] = y1(1)
     for h in range(2):
         e = ts(T["yo%d" % h][:], T["ps%d" % h][:, 0:32], 4096.0, A.mult, -float(KC), A.add, res[h])

import math
import numpy as np
from concourse.bass import DstId, RemoteDMATransfer
from concourse.mybir import AluOpType as A, ActivationFunctionType as F, AxisListType as AX

NR, ST = 4, 8
KC = 30718 - 2048
BIG = 12582912.0
SCRATCH = {
    "Xb": ("sbuf", [128, 4096], "bfloat16"), "Xe": ("sbuf", [128, 4096], "bfloat16"),
    "V": ("sbuf", [128, 16392], "int32"), "W": ("sbuf", [128, 13312], "float32"), "wi": ("sbuf", [128, 2048], "int32"),
    "vl": ("sbuf", [128, 1024], "uint16"),
    "q0": ("sbuf", [128, 256], "uint16"), "q1": ("sbuf", [128, 256], "uint16"), "q2": ("sbuf", [128, 256], "uint16"),
    "e0": ("sbuf", [128, 256], "uint16"), "e1": ("sbuf", [128, 256], "uint16"), "e2": ("sbuf", [128, 256], "uint16"),
    "zz": ("sbuf", [128, 16], "float32"), "kt": ("sbuf", [128, 256], "float16"),
    "rt": ("sbuf", [128, 16], "float32"), "inc": ("sbuf", [128, 16], "float32"), "exc": ("sbuf", [128, 16], "float32"),
    "adj": ("sbuf", [128, 4], "float32"),
    "bs": ("sbuf", [128, 264], "float32"),
    "dh": ("sbuf", [128, 264], "float16"), "dr": ("sbuf", [128, 264], "float16"), "de": ("sbuf", [128, 264], "float16"),
    "M1": ("sbuf", [128, 264], "float32"),
    "M0": ("sbuf", [128, 64], "bfloat16"), "km": ("sbuf", [128, 528], "bfloat16"), "jq": ("sbuf", [128, 264], "int32"),
    "xi": ("sbuf", [128, 264], "int32"), "xf": ("sbuf", [128, 264], "float32"), "pi": ("sbuf", [128, 1], "int32"),
    "pk": ("sbuf", [128, 8], "int32"), "pf": ("sbuf", [128, 8], "float32"), "tc": ("sbuf", [128, 40], "float32"),
    "w4": ("sbuf", [128, 1], "float32"),
    "E": ("sbuf", [128, 144], "bfloat16"), "ES": ("sbuf", [128, 144], "float16"),
    "Pm": ("sbuf", [128, 128], "bfloat16"), "Ih": ("sbuf", [128, 128], "float16"), "In": ("sbuf", [128, 128], "float16"),
    "xg": ("sbuf", [128, 128], "int32"), "BO": ("sbuf", [128, 128], "float32"),
    "Lt": ("sbuf", [128, 16], "float32"), "m0i": ("sbuf", [128, 128], "int32"), "m0f": ("sbuf", [128, 128], "float32"),
    "pats_s": ("sbuf", [128, 256], "int32"), "st_s": ("sbuf", [128, 64], "int32"), "cm": ("sbuf", [128, 256], "float32"),
    "cw": ("sbuf", [128, 256], "float32"), "cq": ("sbuf", [128, 256], "float16"), "kd": ("sbuf", [128, 264], "float16"),
    "cz": ("sbuf", [128, 32], "int32"), "st4": ("sbuf", [128, 64], "int32"),
    "psw": ("psum", [128, 512], "float32"), "psh": ("psum", [128, 512], "float32"), "psm": ("psum", [128, 512], "float32"),
    "psd": ("psum", [128, 512], "float32"), "pa": ("psum", [128, 512], "float32"), "pb": ("psum", [128, 512], "float32"),
}
for _k in range(NR):
    SCRATCH["wl%d" % _k] = ("sbuf", [128, 772], "float16")
    SCRATCH["to%d" % _k] = ("sbuf", [128, 4], "float32")
for _k in range(6):
    SCRATCH["dm%d" % _k] = ("sbuf", [128, 128], "float16")
for _h in range(2):
    SCRATCH["ps%d" % _h] = ("psum", [128, 512], "float32")
    SCRATCH["z%d" % _h] = ("sbuf", [128, 32], "int32")
    SCRATCH["la%d" % _h] = ("sbuf", [128, 32], "int32")
    SCRATCH["lb%d" % _h] = ("sbuf", [128, 32], "int32")
    SCRATCH["ua%d" % _h] = ("sbuf", [128, 32], "uint16")
    SCRATCH["ub%d" % _h] = ("sbuf", [128, 32], "uint16")
    SCRATCH["um%d" % _h] = ("sbuf", [128, 32], "uint16")
    SCRATCH["uv%d" % _h] = ("sbuf", [128, 32], "uint16")
    SCRATCH["r0%d" % _h] = ("sbuf", [128, 512], "bfloat16")
    SCRATCH["r1%d" % _h] = ("sbuf", [128, 512], "float32")
    SCRATCH["ya%d" % _h] = ("sbuf", [128, 512], "float16")
    SCRATCH["yb%d" % _h] = ("sbuf", [128, 512], "float16")
    SCRATCH["yo%d" % _h] = ("sbuf", [128, 32], "float32")
SEMAPHORES = ["sv", "sa", "st", "sg", "ls", "gx0", "gx1", "ldp", "yd0", "yd1"] + ["%s%d" % (s, k) for s in "wt" for k in range(NR)] + ["v%d%d" % (k, h) for k in range(NR) for h in range(2)]
SEMAPHORES += ["hin0", "hin1"] + ["%s%d" % (s, k) for s in "xu" for k in range(NR)]
CUT = 257


def helper_of(core, T, topo):
    return [c for c in topo.cores_of(core) if topo.die(c) != topo.die(core) and T.rank_of(c) is None][0]


def write(g, T, topo, cores, mask, ap, sem):
    ids = [DstId(rid=topo.addr(p)[0], pnc=topo.addr(p)[1]) for p in cores]
    g.remote_dma_fused([RemoteDMATransfer(dst_ids=ids, dma_engine_mask=mask, remote_sem=T.sem[sem], srcs=[ap], dsts=[ap for _ in cores])], local_sem=T.sem.ls)
    return bin(mask).count("1")


def words(T, r, h, j=None):
    o = 512 * r + 256 * h
    return T.wi[:, o:o + 256] if j is None else T.wi[:, o + 128 * j:o + 128 * j + 128]


def short(T, r):
    return [T.vl[:, 256 * r:256 * r + 128], T.vl[:, 256 * r + 128:256 * r + 256], T.vl[:, 256 * r:256 * r + 256]]


def handed(T, rank):
    return [(short(T, rank)[2], "v%d1" % rank), (T["wl%d" % rank][:, 0:CUT], "x%d" % rank)]


def inner_mask(core, helper, peer, topo):
    return sum(1 << e for e in [e for e in topo.engines(core, helper) if e not in topo.engines(core, peer)][::2])


def hand_on(g, core, T, topo):
    for rank, owner in enumerate(T.cores):
        if helper_of(owner, T, topo) == core:
            peers = [T.cores[(rank + d) % NR] for d in range(1, NR)]
            n = 0
            for i, (ap, sem) in enumerate(handed(T, rank)):
                g.wait_ge(T.sem["hin%d" % i], bin(inner_mask(owner, core, peers[0], topo)).count("1"))
                n += write(g, T, topo, peers, topo.mask(core, peers[0]), ap, sem)
            g.wait_ge(T.sem.ls, n)


def rank_program(g, core, T, topo):
    rank = T.rank_of(core)
    if rank is None:
        return hand_on(g, core, T, topo)
    peers = [T.cores[(rank + d) % NR] for d in range(1, NR)]
    S = T.sem
    cnt, seen = {"sv": 0, "sa": 0, "st": 0, "sg": 0}, {}

    def waits(q, name, deps):
        for s, n in deps:
            if seen.get((name, s), 0) < n:
                q.wait_ge(S[s], n)
                seen[(name, s)] = n

    def op(q, name, call, args, deps, kw=None):
        waits(q, name, deps)
        call(*args, **(kw or {})).then_inc(S[name], 1)
        cnt[name] += 1
        return (name, cnt[name])

    vec, act, ten, syn = g.vector, g.scalar, g.tensor, g.sync

    def copy(out, in_, *deps):
        return op(vec, "sv", vec.tensor_copy, (out, in_), deps)

    def tt(out, a, b, o, *deps):
        return op(vec, "sv", vec.tensor_tensor, (out, a, b, o), deps)

    def ts(out, a, s1, o1, s2, o2, *deps):
        if o2 is None:
            return op(vec, "sv", vec.tensor_scalar, (out, a, s1, None, o1), deps)
        return op(vec, "sv", vec.tensor_scalar, (out, a, s1, s2, o1, o2), deps)

    def fill(ap, v, *deps):
        return op(vec, "sv", vec.memset, (ap, v), deps)

    def scan(out, a, b, i, *deps):
        return op(vec, "sv", vec.tensor_tensor_scan, (out, a, b, i, A.add, A.subtract), deps)

    def activ(out, in_, f, deps, **kw):
        return op(act, "sa", act.activation, (out, in_, f), deps, kw)

    def affine(out, in_, scale, bias, *deps):
        return activ(out, in_, F.Copy, deps, scale=scale, bias=bias)

    def mms(items, deps):
        waits(ten, "st", deps)
        for i, (out, l, r, a, b) in enumerate(items):
            m = ten.matmul(out, l, r, a, b)
            if i == len(items) - 1:
                m.then_inc(S.st, 1)
        cnt["st"] += 1
        return ("st", cnt["st"])

    op(g, "sg", g.iota, (T.pi[:], [[1, 1]], 0, 1), [])
    for h in range(2):
        g.dma_start(T.Xb[64 * h:64 * h + 64, :], T.bwt[:, 32768 * h:32768 * h + 32768]).then_inc(S["gx%d" % h], 16)
    op(g, "sg", g.iota, (T.V[:, 16384:16392], [[0, 8]], 9, 0), [])
    syn.dma_start(T.pats_s[:], T.pats[:]).then_inc(S.ldp, 16)
    syn.dma_start(T.st_s[:], T.starts[:]).then_inc(S.ldp, 16)

    pk, pf, tc = T.pk, T.pf, T.tc
    mine = T["wl%d" % rank]

    def k1(b, i):
        return b[:, i:i + 1]

    fill(T.km[:, 0:264], 1.0)
    a = fill(T.km[:, 264:528], 0.0)
    for i, (sh, mk) in enumerate([(0, 1), (0, 7), (0, 56), (3, 1), (0, 15), (0, 112), (0, 127), (0, 64)]):
        d = ts(k1(pk, i), T.pi[:], sh, A.logical_shift_right, mk, A.bitwise_and, ("sg", 1))
    dx = scan(T.xf[:], T.km[:, 0:264], T.km[:, 264:528], -1.0, a)
    dp = copy(pf[:, 0:8], pk[:, 0:8], d)
    dw = activ(T.w4[:], k1(pf, 1), F.Exp, [dp], scale=math.log(4.0))
    di = copy(T.xi[:], T.xf[:], dx)
    ts(k1(tc, 3), k1(pf, 2), 2.0, A.mult, 15.0, A.add, dp)
    b = ts(k1(tc, 4), k1(pf, 7), 0.125, A.mult, k1(pf, 1), A.add)
    ts(k1(tc, 5), k1(pf, 5), 15.0, A.add, None, None)
    dI = ts(T.Ih[:], T.xf[:, 0:128], k1(pf, 6), A.is_equal, None, None)
    b = ts(k1(tc, 6), k1(pf, 2), 2.0, A.mult, k1(tc, 4), A.add, b)
    a = ts(T.xg[:], T.xi[:, 0:128], 112, A.bitwise_and, None, None, di)
    c = ts(T.m0i[:, 0:64], T.xi[:, 0:64], 2, A.logical_shift_right, None, None)
    d = ts(T.m0i[:, 64:128], T.xi[:, 0:64], 3, A.bitwise_and, None, None)
    dP = ts(T.Pm[:], T.xf[:, 0:128], k1(tc, 6), A.is_equal, None, None, b)
    ts(T.BO[:], T.xg[:], k1(pf, 5), A.is_equal, 1.0 / 2048, A.mult, a)
    c = ts(T.m0f[:, 0:64], T.m0i[:, 0:64], k1(pf, 4), A.is_gt, None, None, d)
    d = ts(T.m0f[:, 64:128], T.m0i[:, 64:128], 1.0, A.add, None, None)
    ts(T.ES[:], T.xf[:, 0:144], k1(tc, 5), A.is_equal, 2.0 ** -12, A.mult)
    a = tt(T.m0f[:, 0:64], T.m0f[:, 0:64], T.m0f[:, 64:128], A.mult, d)
    ts(T.Lt[:], T.xf[:, 0:16], k1(pf, 4), A.is_gt, None, None)
    ts(T.jq[:], T.xi[:], 15, A.bitwise_and, None, None)
    d0 = ts(T.M0[:], T.m0f[:, 0:64], -1.0, A.add, None, None, a)
    dE = ts(T.E[:], T.xf[:, 0:144], k1(tc, 3), A.is_equal, T.w4[:], A.mult, dw)

    def parts(h, *deps):
        return ts(T["lb%d" % h][:], T["z%d" % h][:], 6, A.logical_shift_right, 0x30FF, A.bitwise_and, *deps)

    def list_w(h, t, *deps):
        return tt(T["ub%d" % h][:], T["lb%d" % h][:], T.cw[:, 32 * t:32 * t + 32], A.add, *deps)

    def list_q(h, *deps):
        return ts(T["la%d" % h][:], T["z%d" % h][:], 63, A.bitwise_and, None, None, *deps)

    def list0(h, l):
        return activ(T["ua%d" % h][:], T["la%d" % h][:], F.Copy, [l])

    def mask0(h, u, *deps):
        return activ(T["r0%d" % h][:], T.M0[:].indirect(T["ua%d" % h][:]), F.Copy, [u] + list(deps))

    def mask1(h, m, *deps):
        return activ(T["r1%d" % h][:], T.M1[:, 0:257].indirect(T["um%d" % h][:]), F.Copy, [m] + list(deps))

    affine(T.st4[:], T.st_s[:], 4.0, 0.0, ("ldp", 32))
    dK = affine(T.cz[:], T.pats_s[:, 0:32], 1048577.0, 0.0)
    for h in range(2):
        affine(T["uv%d" % h][:], T.st_s[:, 32 * h:32 * h + 32], 1.0 / 16, -15.0 / 32)
    affine(T.cq[:], T.pats_s[:], 2.0 ** -14, 0.0)
    zr = [tt(T["z%d" % h][:], T.st4[:, 32 * h:32 * h + 32], T.cz[:], A.add, dK) for h in range(2)]
    dC = ts(T.cw[:], T.pats_s[:], 256.0, A.mult, None, None)
    la = [list_q(h, zr[h]) for h in range(2)]
    pb = [parts(h) for h in range(2)]
    u = [list0(h, la[h]) for h in range(2)]
    um = [affine(T["um%d" % h][:], T["z%d" % h][:], 2.0 ** -14, 2.0 ** -15 - 0.5) for h in range(2)]
    mk = [[mask0(0, u[0], d0), None], [None, None]]
    ts(T.In[:], T.Ih[:], -1.0, A.mult, None, None)
    fill(T.e0[:], 0)
    lb = [list_w(h, 0, pb[h], dC) for h in range(2)]

    ts(k1(tc, 8), k1(pf, 3), -448.0, A.mult, 448.0, A.add)
    for i, v in enumerate([9, 8]):
        ts(k1(tc, 10 + i), k1(pf, 4), float(v), A.is_equal, 256.0, A.mult)
    for i, v in enumerate([11, 10, 13, 12]):
        a = ts(k1(tc, 12 + i), k1(pf, 4), float(v), A.is_equal, None, None)
    ts(T.kd[:], T.jq[:], k1(pf, 4), A.is_equal, -6144.0, A.mult, d0)
    b = tt(k1(tc, 18), k1(tc, 8), k1(pf, 0), A.mult, a)
    c = ts(tc[:, 22:24], tc[:, 12:14], -2048.0, A.mult, 2048.0, A.add)
    d = ts(tc[:, 24:26], tc[:, 14:16], 2046.0, A.mult, None, None)
    b = tt(k1(tc, 19), k1(tc, 8), k1(tc, 18), A.subtract, b)
    tt(tc[:, 26:28], tc[:, 12:14], tc[:, 14:16], A.subtract)
    ts(tc[:, 28:30], tc[:, 14:16], 2048.0, A.mult, None, None)
    b = tt(tc[:, 20:22], tc[:, 18:20], tc[:, 10:12], A.add, b)
    d = tt(tc[:, 22:24], tc[:, 22:24], tc[:, 24:26], A.add, d)
    fill(T.zz[:], 0.0)
    f = ts(tc[:, 30:32], tc[:, 20:22], -1025.0, A.mult, None, None, b)
    ts(mine[:, 0:772:257], T.xi[:, 0:4], 0.0, A.mult, -2048.0, A.add)
    ts(T.adj[:], T.xf[:, 0:4], 3.0, A.is_equal, -2048.0, A.mult)
    tt(tc[:, 32:34], tc[:, 22:24], tc[:, 30:32], A.add, f)

    def later():
        ts(T.kt[:], T.xf[:, 0:256], 16.0, A.mult, -8192.0, A.add)
        for i, col in enumerate([20, 26, 28]):
            for par in range(2):
                ts(T["dm%d" % (2 * i + par)][:], T.Ih[:], k1(tc, col + par), A.mult, None, None)

    ld = [("gx0", 16), ("gx1", 16)]

    packs = {(0, 0): "psw", (0, 1): "psd", (1, 0): "pa", (1, 1): "pb"}
    pkd, at, hd, hist = {}, {}, {}, [T.psh, T.psm]
    for (h, j), bank in packs.items():
        sl = slice(64 * h, 64 * h + 64)
        pkd[h, j] = mms([(T[bank][:, 0:128], T.E[sl, 15 - q:143 - q], T.Xb[sl, 2048 * j + q:2048 * j + 2048:16], q == 0, q == 15) for q in range(16)], [dE, ld[h]])
    for j in range(4):
        sl = slice(1024 * j, 1024 * (j + 1))
        e = activ(T.Xe[:, sl], T.Xb[:, sl], F.Exp, ld, scale=-math.log(32.0))
        hd[j // 2] = mms([(hist[j // 2][:, 64 * (j % 2):64 * (j % 2) + 64], T.Pm[:], T.Xe[:, 1024 * j + q:1024 * (j + 1):16], q == 0, q == 15) for q in range(16)], [dP, e])

    dq = [affine(T["q%d" % c][:, 128:256], hist[1][:, 0:128], 32.0 ** c, -1.0 / 64, hd[1]) for c in range(3)]
    mk[1][0] = mask0(1, u[1])
    affine(T.cm[:], T.pats_s[:], 64.0, 2.0 ** -15 - 0.5 - KC / 4096.0)

    ne = len(topo.engines(core, peers[0]))

    helper, sent = helper_of(core, T, topo), []

    def send(ap, sem, deps):
        waits(g, "gq", deps)
        sent.append(write(g, T, topo, peers, topo.mask(core, peers[0]), ap, sem))

    def hand(i, deps):
        waits(g, "gq", deps)
        sent.append(write(g, T, topo, [helper], inner_mask(core, helper, peers[0], topo), handed(T, rank)[i][0], "hin%d" % i))

    def letter(r, h, k, j=None):
        o = 4096 * r + 2048 * h + 256 * k
        return T.V[:, o:o + 256] if j is None else T.V[:, o + 128 * j:o + 128 * j + 128]

    def there(r, h, j):
        return [at[r, h, i] for i in range(2) if j in (i, None)]

    def unpack(r, h, j, k):
        ts(letter(r, h, k, j), words(T, r, h, j), 2 * k, A.logical_shift_right, 3, A.bitwise_and, *there(r, h, j))

    def top(part):
        for r, h in part:
            e = affine(letter(r, h, 7), words(T, r, h), 2.0 ** -14, 2.0 ** -15 - 0.5, *there(r, h, None))
        return e

    def count(r, c):
        return T["wl%d" % r][:, 257 * c:257 * c + 256]

    def left(r, bank, deps):
        return mms([(T[bank][:, 0:256], T.Ih[:], T.kt[:], True, False)] + [(T[bank][:, 0:256], T.In[:], count(r, c), False, c == 2) for c in range(3)], deps)

    def cols(r, c):
        return T.W[:, 4096 * r + 256 * c:4096 * r + 256 * c + 256]

    def store(r, c, dep):
        waits(g, "gq", [dep])
        return op(g, "sg", g.affine_select, (cols(r, c), count(r, c), [[0, 256]], A.is_ge, 0.0, 0, 0), [])

    def last(r, bank, m):
        return affine(cols(r, 3), T[bank][:, 0:256], 1.0, 0.0, m)

    order = [(rank + NR - k) % NR for k in range(1, NR)]
    come = [(r, h) for h in range(2) for r in order]
    parts_ = [(r, 0, j) for j in range(2) for r in order[:2]] + [(r, h, None) for r, h in come[2:]]
    jobs = [(rank, h, j, k) for h in range(2) for j in range(2) for k in range(7)] + [x + (k,) for x in parts_ for k in range(7)]
    for r in order:
        at.update({(r, 0, 0): ("u%d" % r, ne), (r, 0, 1): ("v%d0" % r, ne), (r, 1, 0): ("v%d1" % r, ne), (r, 1, 1): ("v%d1" % r, ne)})

    def widen(r):
        at[r, 1, 0] = at[r, 1, 1] = affine(words(T, r, 1), short(T, r)[2], 1.0, 0.0, ("v%d1" % r, ne))

    def work(n):
        for job in jobs[:n]:
            unpack(*job)
        del jobs[:n]

    for i, ((h, j), bank) in enumerate(packs.items()):
        at[rank, h, j] = copy(words(T, rank, h, j), T[bank][:, 0:128], pkd[h, j])
        if h == 0:
            send(words(T, rank, 0, j), ("u%d", "v%d0")[j] % rank, [at[rank, 0, j]])
        else:
            a = copy(short(T, rank)[j], T[bank][:, 0:128])
        work(6 if i == 0 else 7)
        if i == 3:
            hand(0, [a])
    later()
    def before(c, j, d):
        return ts(T["e%d" % c][:, 128 * j:128 * j + 128], T["q%d" % (c - 1)][:, 128 * j:128 * j + 128], 32.0, A.mult, None, None, d)

    a = [ts(T["q%d" % c][:, 0:128], hist[0][:, 0:128], 32.0 ** c, A.mult, -1.0 / 64, A.add, hd[0]) for c in range(3)]
    b = [before(c, 0, a[c - 1]) for c in (1, 2)][1]
    work(1 + 6)
    for c in range(3):
        e = before(c + 1, 1, dq[c]) if c < 2 else None
        s = scan(mine[:, 257 * c + 1:257 * c + 257], T["q%d" % c][:], T["e%d" % c][:], -2048.0, dq[c], b)
        if c == 0:
            hand(1, [s])
        b = e
    work(1)
    ts(T["to%d" % rank][:, 0:3], mine[:, 256:771:257], 2048.0, A.add, None, None, s)
    to = op(vec, "sv", vec.tensor_reduce, (T["to%d" % rank][:, 3:4], mine[:, 256:771:257], AX.X, A.add), [], {"negate": True})
    send(T["to%d" % rank][:], "t%d" % rank, [to])
    send(mine[:, CUT:772], "w%d" % rank, [s])
    for c in range(3):
        store(rank, c, s)
    for r in order:
        for c in (1, 2):
            store(r, c, ("w%d" % r, ne))
    for r in order[1:]:
        dG = store(r, 0, ("x%d" % r, ne))

    dL = last(rank, "psw", left(rank, "psw", [s]))
    top([(rank, 0), (rank, 1)] + come[:3])

    banks = dict(zip(order, ("psh", "pa", "pb")))
    work(21 + 2)
    tt(T.rt[:, rank:16:4], T["to%d" % rank][:], T.adj[:], A.add, to)
    for r in order:
        a = tt(T.rt[:, r:16:4], T["to%d" % r][:], T.adj[:], A.add, ("t%d" % r, ne))
    work(1)
    a = scan(T.inc[:], T.rt[:], T.zz[:], 131200.0, a)
    work(1)
    b = copy(T.bs[:, 256:257], T.inc[:, 15:16], a)
    a = tt(T.exc[:], T.inc[:], T.rt[:], A.subtract, a)
    work(1)
    for k in range(16):
        ba = ts(T.bs[:, 16 * k:16 * k + 16], T.Lt[:], k1(T.rt, k), A.mult, k1(T.exc, k), A.add, a)
    widen(order[0])
    widen(order[1])
    n = 257
    m = mms([(T.psm[:, 0:n], T.BO[:], T.bs[:, 0:n], True, True)], [b, ba])
    mms([(T.psd[:, 0:n], T.BO[:], T.bs[:, 0:n], True, False)], [])
    a = affine(T.dh[:, 0:n], T.psm[:, 0:n], 1.0, 2.0 ** -12 - 0.5, m)
    m = mms([(T.psd[:, 0:n], T.In[:], T.dh[:, 0:n], False, True)], [a])
    widen(order[2])
    affine(T.dr[:, 0:n], T.psd[:, 0:n], 1.0, 0.0, m)
    a = affine(T.de[:, 0:n], T.psd[:, 0:n], 2048.0, 2047.75)
    side = [(T.psm[:, 0:129], slice(0, 257, 2)), (T.psw[:, 0:128], slice(1, 256, 2))]
    mp = [mms([(ps, T["dm%d" % (2 * i + par)][:], T[buf][:, sl], i == 0, False) for i, buf in enumerate(("dh", "de", "dr"))] + [(ps, T.Ih[:], T.kd[:, sl], False, True)], [a, dL]) for par, (ps, sl) in enumerate(side)]
    lf = [left(r, banks[r], [("w%d" % r, ne), ("x%d" % r, ne), dq[2]]) for r in order]
    top(come[3:5])
    for par, (ps, sl) in enumerate(side):
        dM = activ(T.M1[:, sl], ps, F.Identity, [mp[par]], bias=k1(tc, 32 + par))
    dT = top(come[5:6])
    mk[0][1] = mask1(0, um[0], dM)
    for i, r in enumerate(order):
        if i < 1:
            affine(cols(r, 0), count(r, 0), 1.0, 0.0, ("x%d" % r, ne))
        dW = last(r, banks[r], lf[i])
    mk[1][1] = mask1(1, um[1], dM)
    work(len(jobs))
    dV = ("sv", cnt["sv"])

    res, du = [None, None], [dT, dT]

    def sums(h, y, nxt, deps):
        ps = T["ps%d" % h][:, 0:32]
        items = [(ps, T.ES[:, 15 - q:143 - q], T[y][:, q::16], nxt is not None and q == 0, nxt is None and q == 15) for q in range(16)]
        if nxt is not None and nxt < ST:
            items.append((ps, T.Ih[:], T.cq[:, 32 * nxt:32 * nxt + 32], False, False))
        return mms(items, deps)

    def y1(h, nxt=None):
        e = tt(T["ya%d" % h][:], T.V[:].indirect(T["uv%d" % h][:]), T["r0%d" % h][:], A.is_equal, du[h], mk[h][0], dV, ("sg", 2))
        return sums(h, "ya%d" % h, nxt, [e])

    def y2(h, nxt=None):
        e = tt(T["yb%d" % h][:], T.W[:].indirect(T["ub%d" % h][:]), T["r1%d" % h][:], A.max, lb[h], mk[h][1], dW, dG)
        return sums(h, "yb%d" % h, nxt, [e, du[h]])

    def head(h, t):
        ps = T["ps%d" % h][:, 0:32]
        z = ts(T["z%d" % h][:], ps, 2.0 ** 14, A.mult, -4.0 * KC, A.add, res[h])
        mk[h][1] = mask1(h, tt(T["um%d" % h][:], ps, T.cm[:, 32 * t:32 * t + 32], A.add))
        b = parts(h, z)
        u = list0(h, list_q(h))
        du[h] = affine(T["uv%d" % h][:], ps, 256.0, 2.0 ** -7 - 0.5 - KC / 16.0)
        mk[h][0] = mask0(h, u)
        res[1 - h] = y1(1 - h)
        lb[h] = list_w(h, t, b)
        y2(h, t + 1)

    y1(0, 1)
    res[0] = y2(0)
    y2(1, 1)
    for t in range(1, ST):
        head(0, t)
        head(1, t)
    res[1] = y1(1)
    for h in range(2):
        e = ts(T["yo%d" % h][:], T["ps%d" % h][:, 0:32], 4096.0, A.mult, -float(KC), A.add, res[h])
        waits(syn, "sy", [e])
        syn.dma_start(T.y[:, 32 * h:32 * h + 32], T["yo%d" % h][:]).then_inc(S["yd%d" % h], 16)
    waits(syn, "sy", [("yd0", 16), ("yd1", 16)])
    g.wait_ge(S.ls, sum(sent))
